import numpy as np, ml_dtypes
CORES = [1,3,5,9,11,13]
N = 6
import mx_ref
NC, G = 512, 2
C = np.float32(0.01674)
BF = ml_dtypes.bfloat16
def cut(t, i, w=512):
    return t[:, w * i:w * i + w]
def tile(rs):
    return np.stack(rs, axis=2).reshape(128, -1).astype(BF)
def layer(w, X):
    out = []
    for i in range(G):
        for t in range(len(X)):
            p = mx_ref.matmul(mx_ref.quantize(cut(w, len(X) * i + t)), X[t])
            z = p if t == 0 else z + p
        out.append(z)
    return out
def act(Z):
    return [np.maximum(s * z, 0) * C for z in Z for s in (1, -1)]
def setup_inputs(rng):
    def f(*shape):
        return mx_ref.flush((rng.standard_normal(shape, dtype=np.float32) * np.exp2(rng.integers(-2, 3, shape[:-1] + (1,)))).astype(BF))
    return {"x": f(N, 128, N * 4 * NC), "w1": f(N, 128, G * 512), "w2": f(N, 128, 2 * 512)}
def setup_inputs_blocks(rng):
    d = setup_inputs(rng)
    for k in ("x", "w1", "w2"): d[k] = mx_ref.spread(d[k], rng, 4)
    return d
def setup_inputs_wide(rng):
    d = setup_inputs(rng)
    for k in ("x", "w1", "w2"): d[k] = mx_ref.flush((d[k].astype(np.float32) * np.exp2(rng.integers(-6, 7, (N, 1, 1))).astype(np.float32)).astype(BF))
    return d
def reference(x, w1, w2, own=None):
    h = np.zeros((N, 128, 4 * NC), BF)
    for c in range(N):
        for j in range(N):
            P = layer(w1[j], [mx_ref.quantize(cut(x[j], c, 4 * NC))])
            Z = P if j == 0 else [z + p for z, p in zip(Z, P)]
        h[c] = tile(act(Z))
    use = h if own is None else own["h"]
    H = [mx_ref.quantize(use[j]) for j in range(N)]
    y = np.zeros((N, 128, NC), np.float32)
    for r in range(N):
        y[r] = mx_ref.matmul(mx_ref.quantize(cut(w2[r], 0)), H[r]) + mx_ref.matmul(mx_ref.quantize(cut(w2[r], 1)), H[(r + 1) % N])
    return {"h": h, "y": y}

@@ -1,0 +1,268 @@
+from concourse.bass import DstId, RemoteDMATransfer
+from concourse.mybir import dt, AluOpType, ActivationFunctionType
+
+SIM_CORES = 16
+NR = 6
+NC = 512
+TW = 4 * NC
+CONST = 0.01674
+
+SCRATCH = {
+    "xb": ("sbuf", [128, NR * TW], "bfloat16"),
+    "xq": ("sbuf", [128, NR * NC], "float8_e4m3fn_x4"),
+    "xs": ("sbuf", [128, NR * NC], "uint8"),
+    "w1b": ("sbuf", [128, 1024], "bfloat16"),
+    "w1q": ("sbuf", [128, 256], "float8_e4m3fn_x4"),
+    "w1s": ("sbuf", [128, 256], "uint8"),
+    "w2b": ("sbuf", [128, 1024], "bfloat16"),
+    "w2q": ("sbuf", [128, 256], "float8_e4m3fn_x4"),
+    "w2s": ("sbuf", [128, 256], "uint8"),
+    "pout": ("sbuf", [128, (NR - 1) * 2 * NC], "float32"),
+    "nr": ("sbuf", [128, 2 * 2 * NC], "float32"),
+    "far": ("sbuf", [128, 2 * NC], "float32"),
+    "zb": ("sbuf", [128, 2 * NC], "float32"),
+    "hb": ("sbuf", [128, TW], "bfloat16"),
+    "hq": ("sbuf", [128, NC], "float8_e4m3fn_x4"),
+    "hs": ("sbuf", [128, NC], "uint8"),
+    "rhq": ("sbuf", [128, NC], "float8_e4m3fn_x4"),
+    "rhs": ("sbuf", [128, NC], "uint8"),
+    "yb": ("sbuf", [128, NC], "float32"),
+    "fl": ("sbuf", [128, 2 * 3 * NC], "float32"),
+    "relq": ("sbuf", [128, NC], "float8_e4m3fn_x4"),
+    "rels": ("sbuf", [128, NC], "uint8"),
+    "ps": ("psum", [128, 8 * NC], "float32"),
+}
+SEMAPHORES = (["lw1", "lw2", "qw1", "qw2", "qh", "va", "z0", "z1", "act", "ha", "mya", "myb", "ye", "yst", "hst",
+               "loc", "gate1", "gate2", "far0", "far1", "nr0", "nr1", "fj0", "fj1", "rl"]
+              + ["lx%d" % c for c in range(NR)] + ["qx%d" % c for c in range(NR)]
+              + ["ma%d" % c for c in range(NR)] + ["mb%d" % c for c in range(NR)] + ["ev%d" % c for c in range(NR)])
+
+
+def _bits(m):
+    return [b for b in range(m.bit_length()) if (m >> b) & 1]
+
+
+def _cnt(m):
+    return len(_bits(m))
+
+
+def _sub(m, part, parts):
+    bs = _bits(m)
+    k = len(bs) // parts
+    return sum(1 << b for b in bs[part * k:(part + 1) * k])
+
+
+def _plan(T, topo):
+    cores = [int(c) for c in T.cores]
+    n = len(cores)
+    chip = [topo.chip(c) for c in cores]
+    prio = set((r + 1) % n for r in range(n) if chip[r] != chip[(r + 1) % n])
+
+    def key(d):
+        return (0 if d in prio else 1, d)
+
+    far = [sorted([d for d in range(n) if chip[d] != chip[r]], key=key) for r in range(n)]
+    near = [sorted([d for d in range(n) if chip[d] == chip[r] and d != r], key=key) for r in range(n)]
+    sends = [far[r] + near[r] for r in range(n)]
+    local, helpers, jobs = {}, {}, {}
+    for ch in sorted(set(chip)):
+        local[ch] = [r for r in range(n) if chip[r] == ch]
+        away = [cores[r] for r in range(n) if chip[r] != ch]
+        hs = [c for c in range(SIM_CORES) if topo.chip(c) == ch and c not in cores
+              and all(topo.may_write(c, a) for a in away)]
+        by = {}
+        for c in hs:
+            by.setdefault(topo.die(c), []).append(c)
+        groups = sorted(by.values(), key=lambda v: -len(v))
+        order = []
+        while any(groups):
+            for v in groups:
+                if v:
+                    order.append(v.pop(0))
+        helpers[ch] = order
+        jobs[ch] = {}
+        for s, d in enumerate(far[local[ch][0]]):
+            for i in range(2):
+                k = 2 * s + i
+                jobs[ch][(d, i)] = (order[k % len(order)], k // len(order))
+    slot = {}
+    for d in range(n):
+        for k, q in enumerate(sorted(near[d], key=lambda q: (sends[q].index(d), q))):
+            slot[(q, d)] = k
+    return {"cores": cores, "n": n, "chip": chip, "prio": prio, "far": far, "near": near, "sends": sends,
+            "local": local, "helpers": helpers, "jobs": jobs, "slot": slot}
+
+
+def _send(g, T, topo, src, dst, out, in_, sem):
+    rid, pid, _se = topo.addr(dst)
+    m = topo.mask(src, dst)
+    g.remote_dma(out_ap=out, in_ap=in_, remote_sem=sem, local_sem=T.sem.loc, pid=pid, routing_id=rid, dma_engine_mask=m)
+    return _cnt(m)
+
+
+def _helper(g, core, T, topo, P):
+    ch = topo.chip(core)
+    if core not in P["helpers"].get(ch, []):
+        return
+    cores, loc = P["cores"], 0
+    mine = sorted([(sl, d, i) for (d, i), (h, sl) in P["jobs"][ch].items() if h == core])
+    ns = len(P["local"][ch])
+    for sl, d, i in mine:
+        g.wait_ge(T.sem["fj%d" % sl], sum(_cnt(_sub(topo.mask(cores[q], core), i, 2)) for q in P["local"][ch]))
+        rid, pid, _se = topo.addr(cores[d])
+        m = topo.mask(core, cores[d])
+        g.remote_dma_fused([RemoteDMATransfer(
+            dst_ids=[DstId(rid=rid, pnc=pid)], dma_engine_mask=m, remote_sem=T.sem["far%d" % i],
+            srcs=[T.fl[:, (sl * ns + q) * NC:(sl * ns + q + 1) * NC] for q in range(ns)],
+            dsts=[T.far[:, i * NC:(i + 1) * NC]], alu_op=1)], local_sem=T.sem.loc)
+        loc += _cnt(m)
+    for s in sorted(P["prio"]):
+        r = (s - 1) % P["n"]
+        if P["chip"][s] != ch or topo.may_write(cores[s], cores[r]):
+            continue
+        hs = P["helpers"][ch]
+        if core == hs[0]:
+            g.wait_ge(T.sem.rl, _cnt(topo.mask(cores[s], core)))
+            loc += _send(g, T, topo, core, cores[r], T.rhq[:].bitcast(dt.uint8), T.relq[:].bitcast(dt.uint8), T.sem.ha)
+        elif core == hs[1]:
+            g.wait_ge(T.sem.rl, _cnt(topo.mask(cores[s], core)))
+            loc += _send(g, T, topo, core, cores[r], T.rhs[:], T.rels[:], T.sem.ha)
+    g.wait_ge(T.sem.loc, loc)
+
+
+def rank_program(g, core, T, topo):
+    P = _plan(T, topo)
+    rank = T.rank_of(core)
+    if rank is None:
+        _helper(g, core, T, topo, P)
+        return
+    cores, n, ch = P["cores"], P["n"], topo.chip(core)
+    sends = P["sends"][rank]
+    order = sends + [rank]
+    sem, V, S, PE, SY = T.sem, g.vector, g.scalar, g.tensor, g.sync
+    Copy, Relu = ActivationFunctionType.Copy, ActivationFunctionType.Relu
+
+    def bank(b):
+        return T.ps[:, b * NC:(b + 1) * NC]
+
+    pair = {c: (k % 3 if c != rank else 3) for k, c in enumerate(order)}
+
+    SY.dma_start(T.w1b[:], T.w1[:, :]).then_inc(sem.lw1, 16)
+    for c in order:
+        SY.dma_start(T.xb[:, c * TW:(c + 1) * TW], T.x[:, c * TW:(c + 1) * TW]).then_inc(sem["lx%d" % c], 16)
+    SY.wait_ge(sem.gate1, 1)
+    SY.dma_start(T.w2b[:], T.w2[:, :]).then_inc(sem.lw2, 16)
+    SY.wait_ge(sem.gate2, 1)
+    SY.wait_ge(sem.act, 4)
+    SY.dma_start(T.h[:, :], T.hb[:]).then_inc(sem.hst, 16)
+    SY.wait_ge(sem.ye, 2)
+    SY.dma_start(T.y[:, :], T.yb[:]).then_inc(sem.yst, 16)
+    SY.wait_ge(sem.hst, 16)
+    SY.wait_ge(sem.yst, 16)
+
+    PE.wait_ge(sem.qw1, 1)
+    for k, c in enumerate(order):
+        PE.wait_ge(sem["qx%d" % c], 1)
+        if c != rank and k >= 3:
+            PE.wait_ge(sem["ev%d" % order[k - 3]], 2)
+        for i, nm in enumerate(("ma", "mb")):
+            PE.matmul_mx(bank(2 * pair[c] + i), T.w1q[:, 128 * i:128 * (i + 1)], T.w1s[:, 128 * i:128 * (i + 1)],
+                         T.xq[:, c * NC:(c + 1) * NC], T.xs[:, c * NC:(c + 1) * NC], True, True
+                         ).then_inc(sem["%s%d" % (nm, c)], 1)
+    yp = 2 * pair[order[2]]
+    PE.wait_ge(sem["ev%d" % order[2]], 2)
+    PE.wait_ge(sem.qh, 1)
+    PE.wait_ge(sem.qw2, 1)
+    HC = NC // 2
+    for a in range(2):
+        PE.matmul_mx(T.ps[:, (yp + a) * NC:(yp + a) * NC + HC], T.w2q[:, 0:128], T.w2s[:, 0:128],
+                     T.hq[:, a * HC:(a + 1) * HC], T.hs[:, a * HC:(a + 1) * HC], True, False)
+    nxt = (rank + 1) % n
+    if topo.may_write(cores[nxt], core):
+        h_in = 2 * _cnt(topo.mask(cores[nxt], core))
+    else:
+        h_in = sum(_cnt(topo.mask(hc, core)) for hc in P["helpers"][P["chip"][nxt]][:2])
+    PE.wait_ge(sem.ha, h_in)
+    for a, nm in enumerate(("mya", "myb")):
+        PE.matmul_mx(T.ps[:, (yp + a) * NC:(yp + a) * NC + HC], T.w2q[:, 128:256], T.w2s[:, 128:256],
+                     T.rhq[:, a * HC:(a + 1) * HC], T.rhs[:, a * HC:(a + 1) * HC], False, True).then_inc(sem[nm], 1)
+
+    for k, c in enumerate(sends):
+        for i, nm in enumerate(("ma", "mb")):
+            S.wait_ge(sem["%s%d" % (nm, c)], 1)
+            S.activation(T.pout[:, (2 * k + i) * NC:(2 * k + i + 1) * NC], bank(2 * pair[c] + i), Copy
+                         ).then_inc(sem["ev%d" % c], 1)
+    S.wait_ge(sem.z0, 1)
+    S.activation(T.hb[:, 0:TW:4], T.zb[:, 0:NC], Relu, scale=CONST).then_inc(sem.act, 1)
+    S.activation(T.hb[:, 1:TW:4], T.zb[:, 0:NC], Relu, scale=-CONST).then_inc(sem.act, 1)
+    S.wait_ge(sem.z1, 1)
+    S.activation(T.hb[:, 2:TW:4], T.zb[:, NC:2 * NC], Relu, scale=CONST).then_inc(sem.act, 1)
+    S.wait_ge(sem.myb, 1)
+    S.activation(T.yb[:, HC:NC], T.ps[:, (yp + 1) * NC:(yp + 1) * NC + HC], Copy).then_inc(sem.ye, 1)
+
+    V.wait_ge(sem.lw1, 16)
+    V.quantize_mx(T.w1q[:], T.w1s[:], T.w1b[:]).then_inc(sem.qw1, 1)
+    for c in order:
+        V.wait_ge(sem["lx%d" % c], 16)
+        V.quantize_mx(T.xq[:, c * NC:(c + 1) * NC], T.xs[:, c * NC:(c + 1) * NC], T.xb[:, c * TW:(c + 1) * TW]
+                      ).then_inc(sem["qx%d" % c], 1)
+    fch = P["chip"][P["far"][rank][0]]
+    for i, nm in enumerate(("ma", "mb")):
+        V.wait_ge(sem["%s%d" % (nm, rank)], 1)
+        V.wait_ge(sem["far%d" % i], _cnt(topo.mask(P["jobs"][fch][(rank, i)][0], core)))
+        V.tensor_tensor(T.zb[:, i * NC:(i + 1) * NC], bank(2 * pair[rank] + i), T.far[:, i * NC:(i + 1) * NC],
+                        AluOpType.add).then_inc(sem.va, 1)
+    by_slot = sorted(P["near"][rank], key=lambda q: P["slot"][(q, rank)])
+    V.wait_ge(sem.nr0, _cnt(topo.mask(cores[by_slot[0]], core)))
+    V.wait_ge(sem.va, 2)
+    for i in range(2):
+        V.tensor_tensor(T.zb[:, i * NC:(i + 1) * NC], T.zb[:, i * NC:(i + 1) * NC], T.nr[:, i * NC:(i + 1) * NC],
+                        AluOpType.add).then_inc(sem.va, 1)
+    V.wait_ge(sem.nr1, _cnt(topo.mask(cores[by_slot[1]], core)))
+    V.wait_ge(sem.va, 4)
+    for i, nm in enumerate(("z0", "z1")):
+        V.tensor_tensor(T.zb[:, i * NC:(i + 1) * NC], T.zb[:, i * NC:(i + 1) * NC],
+                        T.nr[:, (2 + i) * NC:(3 + i) * NC], AluOpType.add).then_inc(sem[nm], 1)
+    V.wait_ge(sem.z1, 1)
+    V.tensor_scalar(T.hb[:, 3:TW:4], T.zb[:, NC:2 * NC], -CONST, 0.0, AluOpType.mult, AluOpType.max
+                    ).then_inc(sem.act, 1)
+    V.wait_ge(sem.act, 4)
+    V.quantize_mx(T.hq[:], T.hs[:], T.hb[:]).then_inc(sem.qh, 1)
+    V.wait_ge(sem.lw2, 16)
+    V.quantize_mx(T.w2q[:], T.w2s[:], T.w2b[:]).then_inc(sem.qw2, 1)
+    V.wait_ge(sem.mya, 1)
+    V.tensor_copy(T.yb[:, 0:HC], T.ps[:, yp * NC:yp * NC + HC]).then_inc(sem.ye, 1)
+
+    loc = 0
+    me = P["local"][ch].index(rank)
+    ns = len(P["local"][ch])
+    for k, c in enumerate(sends):
+        g.wait_ge(sem["ev%d" % c], 2)
+        if P["chip"][c] == ch:
+            sl = P["slot"][(rank, c)]
+            loc += _send(g, T, topo, core, cores[c], T.nr[:, sl * 2 * NC:(sl + 1) * 2 * NC],
+                         T.pout[:, 2 * k * NC:(2 * k + 2) * NC], sem["nr%d" % sl])
+        else:
+            trs = []
+            for i in range(2):
+                hc, sl = P["jobs"][ch][(c, i)]
+                rid, pid, _se = topo.addr(hc)
+                m = _sub(topo.mask(core, hc), i, 2)
+                trs.append(RemoteDMATransfer(
+                    dst_ids=[DstId(rid=rid, pnc=pid)], dma_engine_mask=m, remote_sem=sem["fj%d" % sl],
+                    src=T.pout[:, (2 * k + i) * NC:(2 * k + i + 1) * NC],
+                    dst=T.fl[:, (sl * ns + me) * NC:(sl * ns + me + 1) * NC]))
+                loc += _cnt(m)
+            g.remote_dma_fused(trs, local_sem=sem.loc)
+    g.sem_inc(sem.gate1, 1)
+    g.wait_ge(sem.qh, 1)
+    prv = (rank - 1) % n
+    if topo.may_write(core, cores[prv]):
+        loc += _send(g, T, topo, core, cores[prv], T.rhs[:], T.hs[:], sem.ha)
+        loc += _send(g, T, topo, core, cores[prv], T.rhq[:].bitcast(dt.uint8), T.hq[:].bitcast(dt.uint8), sem.ha)
+    else:
+        hs = P["helpers"][ch]
+        loc += _send(g, T, topo, core, hs[0], T.relq[:].bitcast(dt.uint8), T.hq[:].bitcast(dt.uint8), sem.rl)
+        loc += _send(g, T, topo, core, hs[1], T.rels[:], T.hs[:], sem.rl)
+    g.sem_inc(sem.gate2, 1)
+    g.wait_ge(sem.loc, loc)

@@ -4,6 +4,7 @@ from concourse.mybir import dt, AluOpType, ActivationFunctionType
 SIM_CORES = 16
 NR = 6
 NC = 512
+HC = NC // 2
 TW = 4 * NC
 CONST = 0.01674
 
@@ -17,8 +18,11 @@ SCRATCH = {
     "w2b": ("sbuf", [128, 1024], "bfloat16"),
     "w2q": ("sbuf", [128, 256], "float8_e4m3fn_x4"),
     "w2s": ("sbuf", [128, 256], "uint8"),
-    "pout": ("sbuf", [128, (NR - 1) * 2 * NC], "float32"),
-    "nr": ("sbuf", [128, 2 * 2 * NC], "float32"),
+    "pout": ("sbuf", [128, 3 * 2 * NC], "float32"),
+    "rwq": ("sbuf", [128, 2 * 256], "float8_e4m3fn_x4"),
+    "rws": ("sbuf", [128, 2 * 256], "uint8"),
+    "rxq": ("sbuf", [128, 2 * NC], "float8_e4m3fn_x4"),
+    "rxs": ("sbuf", [128, 2 * NC], "uint8"),
     "far": ("sbuf", [128, 2 * NC], "float32"),
     "zb": ("sbuf", [128, 2 * NC], "float32"),
     "hb": ("sbuf", [128, TW], "bfloat16"),
@@ -32,8 +36,8 @@ SCRATCH = {
     "rels": ("sbuf", [128, NC], "uint8"),
     "ps": ("psum", [128, 8 * NC], "float32"),
 }
-SEMAPHORES = (["lw1", "lw2", "qw1", "qw2", "qh", "va", "z0", "z1", "act", "ha", "mya", "myb", "ye", "yst", "hst",
-               "loc", "gate1", "gate2", "far0", "far1", "nr0", "nr1", "fj0", "fj1", "rl"]
+SEMAPHORES = (["lw1", "lw2", "qw1", "qw2", "qh", "z0", "z1", "act", "ha", "mya", "myb", "ye", "yst", "hst",
+               "loc", "gate1", "gate2", "far0", "far1", "aw", "ax0", "ax1", "fj0", "fj1", "rl", "mza", "mzb"]
               + ["lx%d" % c for c in range(NR)] + ["qx%d" % c for c in range(NR)]
               + ["ma%d" % c for c in range(NR)] + ["mb%d" % c for c in range(NR)] + ["ev%d" % c for c in range(NR)])
 
@@ -63,7 +67,6 @@ def _plan(T, topo):
 
     far = [sorted([d for d in range(n) if chip[d] != chip[r]], key=key) for r in range(n)]
     near = [sorted([d for d in range(n) if chip[d] == chip[r] and d != r], key=key) for r in range(n)]
-    sends = [far[r] + near[r] for r in range(n)]
     local, helpers, jobs = {}, {}, {}
     for ch in sorted(set(chip)):
         local[ch] = [r for r in range(n) if chip[r] == ch]
@@ -87,9 +90,9 @@ def _plan(T, topo):
                 jobs[ch][(d, i)] = (order[k % len(order)], k // len(order))
     slot = {}
     for d in range(n):
-        for k, q in enumerate(sorted(near[d], key=lambda q: (sends[q].index(d), q))):
+        for k, q in enumerate(sorted(near[d], key=lambda q: (1 if q in prio else 0, q))):
             slot[(q, d)] = k
-    return {"cores": cores, "n": n, "chip": chip, "prio": prio, "far": far, "near": near, "sends": sends,
+    return {"cores": cores, "n": n, "chip": chip, "prio": prio, "far": far, "near": near,
             "local": local, "helpers": helpers, "jobs": jobs, "slot": slot}
 
 
@@ -98,6 +101,10 @@ def _send(g, T, topo, src, dst, out, in_, sem):
     m = topo.mask(src, dst)
     g.remote_dma(out_ap=out, in_ap=in_, remote_sem=sem, local_sem=T.sem.loc, pid=pid, routing_id=rid, dma_engine_mask=m)
     return _cnt(m)
+
+
+def _u8(view):
+    return view.bitcast(dt.uint8)
 
 
 def _helper(g, core, T, topo, P):
@@ -120,11 +127,12 @@ def _helper(g, core, T, topo, P):
         r = (s - 1) % P["n"]
         if P["chip"][s] != ch or topo.may_write(cores[s], cores[r]):
             continue
-        hs = P["helpers"][ch]
-        if core == hs[0]:
-            g.wait_ge(T.sem.rl, _cnt(topo.mask(cores[s], core)))
-            loc += _send(g, T, topo, core, cores[r], T.rhq[:].bitcast(dt.uint8), T.relq[:].bitcast(dt.uint8), T.sem.ha)
-        elif core == hs[1]:
+        k = P["helpers"][ch].index(core)
+        if k < 2:
+            g.wait_ge(T.sem.rl, _cnt(_sub(topo.mask(cores[s], core), k, 2)))
+            loc += _send(g, T, topo, core, cores[r], _u8(T.rhq[:, k * HC:(k + 1) * HC]),
+                         _u8(T.relq[:, k * HC:(k + 1) * HC]), T.sem.ha)
+        elif k == 2:
             g.wait_ge(T.sem.rl, _cnt(topo.mask(cores[s], core)))
             loc += _send(g, T, topo, core, cores[r], T.rhs[:], T.rels[:], T.sem.ha)
     g.wait_ge(T.sem.loc, loc)
@@ -137,18 +145,22 @@ def rank_program(g, core, T, topo):
         _helper(g, core, T, topo, P)
         return
     cores, n, ch = P["cores"], P["n"], topo.chip(core)
-    sends = P["sends"][rank]
-    order = sends + [rank]
+    far, near = P["far"][rank], P["near"][rank]
+    early = rank in P["prio"]
     sem, V, S, PE, SY = T.sem, g.vector, g.scalar, g.tensor, g.sync
     Copy, Relu = ActivationFunctionType.Copy, ActivationFunctionType.Relu
+    order = far + [rank] + near if early else far + near + [rank]
 
     def bank(b):
         return T.ps[:, b * NC:(b + 1) * NC]
 
-    pair = {c: (k % 3 if c != rank else 3) for k, c in enumerate(order)}
+    def xcol(t, c):
+        return t[:, c * NC:(c + 1) * NC]
 
     SY.dma_start(T.w1b[:], T.w1[:, :]).then_inc(sem.lw1, 16)
     for c in order:
+        if c == rank and not early:
+            SY.wait_ge(sem.gate1, 1)
         SY.dma_start(T.xb[:, c * TW:(c + 1) * TW], T.x[:, c * TW:(c + 1) * TW]).then_inc(sem["lx%d" % c], 16)
     SY.wait_ge(sem.gate1, 1)
     SY.dma_start(T.w2b[:], T.w2[:, :]).then_inc(sem.lw2, 16)
@@ -161,19 +173,32 @@ def rank_program(g, core, T, topo):
     SY.wait_ge(sem.yst, 16)
 
     PE.wait_ge(sem.qw1, 1)
-    for k, c in enumerate(order):
+    for k, c in enumerate(far):
         PE.wait_ge(sem["qx%d" % c], 1)
-        if c != rank and k >= 3:
-            PE.wait_ge(sem["ev%d" % order[k - 3]], 2)
         for i, nm in enumerate(("ma", "mb")):
-            PE.matmul_mx(bank(2 * pair[c] + i), T.w1q[:, 128 * i:128 * (i + 1)], T.w1s[:, 128 * i:128 * (i + 1)],
-                         T.xq[:, c * NC:(c + 1) * NC], T.xs[:, c * NC:(c + 1) * NC], True, True
-                         ).then_inc(sem["%s%d" % (nm, c)], 1)
-    yp = 2 * pair[order[2]]
-    PE.wait_ge(sem["ev%d" % order[2]], 2)
+            PE.matmul_mx(bank(2 * k + i), T.w1q[:, 128 * i:128 * (i + 1)], T.w1s[:, 128 * i:128 * (i + 1)],
+                         xcol(T.xq, c), xcol(T.xs, c), True, True).then_inc(sem["%s%d" % (nm, c)], 1)
+    by_slot = sorted(near, key=lambda q: P["slot"][(q, rank)])
+    terms = (["own", 0, 1] if early else [0, 1, "own"])
+    for t, what in enumerate(terms):
+        if what == "own":
+            PE.wait_ge(sem["qx%d" % rank], 1)
+            wq, ws, xq, xs = T.w1q, T.w1s, xcol(T.xq, rank), xcol(T.xs, rank)
+            w0 = 0
+        else:
+            PE.wait_ge(sem.aw, sum(2 * _cnt(topo.mask(cores[q], core)) for q in near))
+            PE.wait_ge(sem["ax%d" % what], 2 * _cnt(topo.mask(cores[by_slot[what]], core)))
+            wq, ws, xq, xs = T.rwq, T.rws, xcol(T.rxq, what), xcol(T.rxs, what)
+            w0 = 256 * what
+        for i, nm in enumerate(("mza", "mzb")):
+            mm = PE.matmul_mx(bank(6 + i), wq[:, w0 + 128 * i:w0 + 128 * (i + 1)], ws[:, w0 + 128 * i:w0 + 128 * (i + 1)],
+                              xq, xs, t == 0, t == 2)
+            if t == 2:
+                mm.then_inc(sem[nm], 1)
+    yp = 4
+    PE.wait_ge(sem["ev%d" % far[2]], 2)
     PE.wait_ge(sem.qh, 1)
     PE.wait_ge(sem.qw2, 1)
-    HC = NC // 2
     for a in range(2):
         PE.matmul_mx(T.ps[:, (yp + a) * NC:(yp + a) * NC + HC], T.w2q[:, 0:128], T.w2s[:, 0:128],
                      T.hq[:, a * HC:(a + 1) * HC], T.hs[:, a * HC:(a + 1) * HC], True, False)
@@ -181,16 +206,16 @@ def rank_program(g, core, T, topo):
     if topo.may_write(cores[nxt], core):
         h_in = 2 * _cnt(topo.mask(cores[nxt], core))
     else:
-        h_in = sum(_cnt(topo.mask(hc, core)) for hc in P["helpers"][P["chip"][nxt]][:2])
+        h_in = sum(_cnt(topo.mask(hc, core)) for hc in P["helpers"][P["chip"][nxt]][:3])
     PE.wait_ge(sem.ha, h_in)
     for a, nm in enumerate(("mya", "myb")):
         PE.matmul_mx(T.ps[:, (yp + a) * NC:(yp + a) * NC + HC], T.w2q[:, 128:256], T.w2s[:, 128:256],
                      T.rhq[:, a * HC:(a + 1) * HC], T.rhs[:, a * HC:(a + 1) * HC], False, True).then_inc(sem[nm], 1)
 
-    for k, c in enumerate(sends):
+    for k, c in enumerate(far):
         for i, nm in enumerate(("ma", "mb")):
             S.wait_ge(sem["%s%d" % (nm, c)], 1)
-            S.activation(T.pout[:, (2 * k + i) * NC:(2 * k + i + 1) * NC], bank(2 * pair[c] + i), Copy
+            S.activation(T.pout[:, (2 * k + i) * NC:(2 * k + i + 1) * NC], bank(2 * k + i), Copy
                          ).then_inc(sem["ev%d" % c], 1)
     S.wait_ge(sem.z0, 1)
     S.activation(T.hb[:, 0:TW:4], T.zb[:, 0:NC], Relu, scale=CONST).then_inc(sem.act, 1)
@@ -204,25 +229,13 @@ def rank_program(g, core, T, topo):
     V.quantize_mx(T.w1q[:], T.w1s[:], T.w1b[:]).then_inc(sem.qw1, 1)
     for c in order:
         V.wait_ge(sem["lx%d" % c], 16)
-        V.quantize_mx(T.xq[:, c * NC:(c + 1) * NC], T.xs[:, c * NC:(c + 1) * NC], T.xb[:, c * TW:(c + 1) * TW]
-                      ).then_inc(sem["qx%d" % c], 1)
-    fch = P["chip"][P["far"][rank][0]]
-    for i, nm in enumerate(("ma", "mb")):
-        V.wait_ge(sem["%s%d" % (nm, rank)], 1)
+        V.quantize_mx(xcol(T.xq, c), xcol(T.xs, c), T.xb[:, c * TW:(c + 1) * TW]).then_inc(sem["qx%d" % c], 1)
+    fch = P["chip"][far[0]]
+    for i, (nm, zn) in enumerate((("mza", "z0"), ("mzb", "z1"))):
         V.wait_ge(sem["far%d" % i], _cnt(topo.mask(P["jobs"][fch][(rank, i)][0], core)))
-        V.tensor_tensor(T.zb[:, i * NC:(i + 1) * NC], bank(2 * pair[rank] + i), T.far[:, i * NC:(i + 1) * NC],
-                        AluOpType.add).then_inc(sem.va, 1)
-    by_slot = sorted(P["near"][rank], key=lambda q: P["slot"][(q, rank)])
-    V.wait_ge(sem.nr0, _cnt(topo.mask(cores[by_slot[0]], core)))
-    V.wait_ge(sem.va, 2)
-    for i in range(2):
-        V.tensor_tensor(T.zb[:, i * NC:(i + 1) * NC], T.zb[:, i * NC:(i + 1) * NC], T.nr[:, i * NC:(i + 1) * NC],
-                        AluOpType.add).then_inc(sem.va, 1)
-    V.wait_ge(sem.nr1, _cnt(topo.mask(cores[by_slot[1]], core)))
-    V.wait_ge(sem.va, 4)
-    for i, nm in enumerate(("z0", "z1")):
-        V.tensor_tensor(T.zb[:, i * NC:(i + 1) * NC], T.zb[:, i * NC:(i + 1) * NC],
-                        T.nr[:, (2 + i) * NC:(3 + i) * NC], AluOpType.add).then_inc(sem[nm], 1)
+        V.wait_ge(sem[nm], 1)
+        V.tensor_tensor(T.zb[:, i * NC:(i + 1) * NC], bank(6 + i), T.far[:, i * NC:(i + 1) * NC],
+                        AluOpType.add).then_inc(sem[zn], 1)
     V.wait_ge(sem.z1, 1)
     V.tensor_scalar(T.hb[:, 3:TW:4], T.zb[:, NC:2 * NC], -CONST, 0.0, AluOpType.mult, AluOpType.max
                     ).then_inc(sem.act, 1)
@@ -236,33 +249,49 @@ def rank_program(g, core, T, topo):
     loc = 0
     me = P["local"][ch].index(rank)
     ns = len(P["local"][ch])
-    for k, c in enumerate(sends):
+    for k, c in enumerate(far):
         g.wait_ge(sem["ev%d" % c], 2)
-        if P["chip"][c] == ch:
-            sl = P["slot"][(rank, c)]
-            loc += _send(g, T, topo, core, cores[c], T.nr[:, sl * 2 * NC:(sl + 1) * 2 * NC],
-                         T.pout[:, 2 * k * NC:(2 * k + 2) * NC], sem["nr%d" % sl])
-        else:
-            trs = []
-            for i in range(2):
-                hc, sl = P["jobs"][ch][(c, i)]
-                rid, pid, _se = topo.addr(hc)
-                m = _sub(topo.mask(core, hc), i, 2)
-                trs.append(RemoteDMATransfer(
-                    dst_ids=[DstId(rid=rid, pnc=pid)], dma_engine_mask=m, remote_sem=sem["fj%d" % sl],
-                    src=T.pout[:, (2 * k + i) * NC:(2 * k + i + 1) * NC],
-                    dst=T.fl[:, (sl * ns + me) * NC:(sl * ns + me + 1) * NC]))
-                loc += _cnt(m)
-            g.remote_dma_fused(trs, local_sem=sem.loc)
+        trs = []
+        for i in range(2):
+            hc, sl = P["jobs"][ch][(c, i)]
+            rid, pid, _se = topo.addr(hc)
+            m = _sub(topo.mask(core, hc), i, 2)
+            trs.append(RemoteDMATransfer(
+                dst_ids=[DstId(rid=rid, pnc=pid)], dma_engine_mask=m, remote_sem=sem["fj%d" % sl],
+                src=T.pout[:, (2 * k + i) * NC:(2 * k + i + 1) * NC],
+                dst=T.fl[:, (sl * ns + me) * NC:(sl * ns + me + 1) * NC]))
+            loc += _cnt(m)
+        g.remote_dma_fused(trs, local_sem=sem.loc)
+    ids = [DstId(rid=topo.addr(cores[q])[0], pnc=topo.addr(cores[q])[1]) for q in near]
+    wm = topo.mask(core, cores[near[0]])
+    cols = [256 * P["slot"][(rank, q)] for q in near]
+    g.wait_ge(sem.qw1, 1)
+    g.remote_dma_fused([RemoteDMATransfer(dst_ids=ids, dma_engine_mask=wm, remote_sem=sem.aw, srcs=[_u8(T.w1q[:])],
+                                          dsts=[_u8(T.rwq[:, a:a + 256]) for a in cols])], local_sem=sem.loc)
+    g.remote_dma_fused([RemoteDMATransfer(dst_ids=ids, dma_engine_mask=wm, remote_sem=sem.aw, srcs=[T.w1s[:]],
+                                          dsts=[T.rws[:, a:a + 256] for a in cols])], local_sem=sem.loc)
+    loc += 2 * _cnt(wm)
+    for c in near:
+        sl = P["slot"][(rank, c)]
+        g.wait_ge(sem["qx%d" % c], 1)
+        loc += _send(g, T, topo, core, cores[c], _u8(xcol(T.rxq, sl)), _u8(xcol(T.xq, c)), sem["ax%d" % sl])
+        loc += _send(g, T, topo, core, cores[c], xcol(T.rxs, sl), xcol(T.xs, c), sem["ax%d" % sl])
     g.sem_inc(sem.gate1, 1)
     g.wait_ge(sem.qh, 1)
     prv = (rank - 1) % n
     if topo.may_write(core, cores[prv]):
         loc += _send(g, T, topo, core, cores[prv], T.rhs[:], T.hs[:], sem.ha)
-        loc += _send(g, T, topo, core, cores[prv], T.rhq[:].bitcast(dt.uint8), T.hq[:].bitcast(dt.uint8), sem.ha)
+        loc += _send(g, T, topo, core, cores[prv], _u8(T.rhq[:]), _u8(T.hq[:]), sem.ha)
     else:
         hs = P["helpers"][ch]
-        loc += _send(g, T, topo, core, hs[0], T.relq[:].bitcast(dt.uint8), T.hq[:].bitcast(dt.uint8), sem.rl)
-        loc += _send(g, T, topo, core, hs[1], T.rels[:], T.hs[:], sem.rl)
+        trs = []
+        for k in range(2):
+            rid, pid, _se = topo.addr(hs[k])
+            m = _sub(topo.mask(core, hs[k]), k, 2)
+            trs.append(RemoteDMATransfer(dst_ids=[DstId(rid=rid, pnc=pid)], dma_engine_mask=m, remote_sem=sem.rl,
+                                         src=_u8(T.hq[:, k * HC:(k + 1) * HC]), dst=_u8(T.relq[:, k * HC:(k + 1) * HC])))
+            loc += _cnt(m)
+        g.remote_dma_fused(trs, local_sem=sem.loc)
+        loc += _send(g, T, topo, core, hs[2], T.rels[:], T.hs[:], sem.rl)
     g.sem_inc(sem.gate2, 1)
     g.wait_ge(sem.loc, loc)

@@ -5,6 +5,7 @@ SIM_CORES = 16
 NR = 6
 NC = 512
 HC = NC // 2
+NW = 256
 TW = 4 * NC
 CONST = 0.01674
 
@@ -13,16 +14,14 @@ SCRATCH = {
     "xq": ("sbuf", [128, NR * NC], "float8_e4m3fn_x4"),
     "xs": ("sbuf", [128, NR * NC], "uint8"),
     "w1b": ("sbuf", [128, 1024], "bfloat16"),
-    "w1q": ("sbuf", [128, 256], "float8_e4m3fn_x4"),
-    "w1s": ("sbuf", [128, 256], "uint8"),
+    "nq": ("sbuf", [128, 2 * NC + NW], "float8_e4m3fn_x4"),
+    "ns": ("sbuf", [128, 2 * NC + NW], "uint8"),
     "w2b": ("sbuf", [128, 1024], "bfloat16"),
     "w2q": ("sbuf", [128, 256], "float8_e4m3fn_x4"),
     "w2s": ("sbuf", [128, 256], "uint8"),
     "pout": ("sbuf", [128, 3 * 2 * NC], "float32"),
-    "rwq": ("sbuf", [128, 2 * 256], "float8_e4m3fn_x4"),
-    "rws": ("sbuf", [128, 2 * 256], "uint8"),
-    "rxq": ("sbuf", [128, 2 * NC], "float8_e4m3fn_x4"),
-    "rxs": ("sbuf", [128, 2 * NC], "uint8"),
+    "rq": ("sbuf", [128, 2 * (NC + NW)], "float8_e4m3fn_x4"),
+    "rs": ("sbuf", [128, 2 * (NC + NW)], "uint8"),
     "far": ("sbuf", [128, 2 * NC], "float32"),
     "zb": ("sbuf", [128, 2 * NC], "float32"),
     "hb": ("sbuf", [128, TW], "bfloat16"),
@@ -34,10 +33,13 @@ SCRATCH = {
     "fl": ("sbuf", [128, 2 * 3 * NC], "float32"),
     "relq": ("sbuf", [128, NC], "float8_e4m3fn_x4"),
     "rels": ("sbuf", [128, NC], "uint8"),
+    "hwq": ("sbuf", [128, NW], "float8_e4m3fn_x4"),
+    "hws": ("sbuf", [128, NW], "uint8"),
     "ps": ("psum", [128, 8 * NC], "float32"),
 }
 SEMAPHORES = (["lw1", "lw2", "qw1", "qw2", "qh", "z0", "z1", "act", "ha", "mya", "myb", "ye", "yst", "hst",
-               "loc", "gate1", "gate2", "far0", "far1", "aw", "ax0", "ax1", "fj0", "fj1", "rl", "mza", "mzb"]
+               "loc", "gate0", "gatef", "gate1", "gate2", "far0", "far1", "aw", "wr", "ax0", "ax1", "fj0", "fj1", "rl",
+               "mza", "mzb"]
               + ["lx%d" % c for c in range(NR)] + ["qx%d" % c for c in range(NR)]
               + ["ma%d" % c for c in range(NR)] + ["mb%d" % c for c in range(NR)] + ["ev%d" % c for c in range(NR)])
 
@@ -114,6 +116,19 @@ def _helper(g, core, T, topo, P):
     cores, loc = P["cores"], 0
     mine = sorted([(sl, d, i) for (d, i), (h, sl) in P["jobs"][ch].items() if h == core])
     ns = len(P["local"][ch])
+    k = P["helpers"][ch].index(core)
+    if k < ns:
+        q = P["local"][ch][k]
+        g.wait_ge(T.sem.wr, 2 * _cnt(topo.mask(cores[q], core)))
+        ds = P["near"][q]
+        ids = [DstId(rid=topo.addr(cores[d])[0], pnc=topo.addr(cores[d])[1]) for d in ds]
+        m = topo.mask(core, cores[ds[0]])
+        cols = [P["slot"][(q, d)] * (NC + NW) + NC for d in ds]
+        g.remote_dma_fused([RemoteDMATransfer(dst_ids=ids, dma_engine_mask=m, remote_sem=T.sem.aw, srcs=[_u8(T.hwq[:])],
+                                              dsts=[_u8(T.rq[:, a:a + NW]) for a in cols])], local_sem=T.sem.loc)
+        g.remote_dma_fused([RemoteDMATransfer(dst_ids=ids, dma_engine_mask=m, remote_sem=T.sem.aw, srcs=[T.hws[:]],
+                                              dsts=[T.rs[:, a:a + NW] for a in cols])], local_sem=T.sem.loc)
+        loc += 2 * _cnt(m)
     for sl, d, i in mine:
         g.wait_ge(T.sem["fj%d" % sl], sum(_cnt(_sub(topo.mask(cores[q], core), i, 2)) for q in P["local"][ch]))
         rid, pid, _se = topo.addr(cores[d])
@@ -127,7 +142,6 @@ def _helper(g, core, T, topo, P):
         r = (s - 1) % P["n"]
         if P["chip"][s] != ch or topo.may_write(cores[s], cores[r]):
             continue
-        k = P["helpers"][ch].index(core)
         if k < 2:
             g.wait_ge(T.sem.rl, _cnt(_sub(topo.mask(cores[s], core), k, 2)))
             loc += _send(g, T, topo, core, cores[r], _u8(T.rhq[:, k * HC:(k + 1) * HC]),
@@ -149,7 +163,8 @@ def rank_program(g, core, T, topo):
     early = rank in P["prio"]
     sem, V, S, PE, SY = T.sem, g.vector, g.scalar, g.tensor, g.sync
     Copy, Relu = ActivationFunctionType.Copy, ActivationFunctionType.Relu
-    order = far + [rank] + near if early else far + near + [rank]
+    fourth, rest = (rank, near) if early else (near[0], [near[1], rank])
+    order = far + [fourth] + rest
 
     def bank(b):
         return T.ps[:, b * NC:(b + 1) * NC]
@@ -157,10 +172,18 @@ def rank_program(g, core, T, topo):
     def xcol(t, c):
         return t[:, c * NC:(c + 1) * NC]
 
+    def tile(c):
+        if c in near:
+            a = near.index(c) * (NC + NW)
+            return T.nq[:, a:a + NC], T.ns[:, a:a + NC]
+        return xcol(T.xq, c), xcol(T.xs, c)
+
     SY.dma_start(T.w1b[:], T.w1[:, :]).then_inc(sem.lw1, 16)
     for c in order:
-        if c == rank and not early:
-            SY.wait_ge(sem.gate1, 1)
+        if c == fourth:
+            SY.wait_ge(sem.gate0, 1)
+        if c == rest[0]:
+            SY.wait_ge(sem.gatef, 1)
         SY.dma_start(T.xb[:, c * TW:(c + 1) * TW], T.x[:, c * TW:(c + 1) * TW]).then_inc(sem["lx%d" % c], 16)
     SY.wait_ge(sem.gate1, 1)
     SY.dma_start(T.w2b[:], T.w2[:, :]).then_inc(sem.lw2, 16)
@@ -176,20 +199,22 @@ def rank_program(g, core, T, topo):
     for k, c in enumerate(far):
         PE.wait_ge(sem["qx%d" % c], 1)
         for i, nm in enumerate(("ma", "mb")):
-            PE.matmul_mx(bank(2 * k + i), T.w1q[:, 128 * i:128 * (i + 1)], T.w1s[:, 128 * i:128 * (i + 1)],
+            PE.matmul_mx(bank(2 * k + i), T.nq[:, NC + 128 * i:NC + 128 * (i + 1)], T.ns[:, NC + 128 * i:NC + 128 * (i + 1)],
                          xcol(T.xq, c), xcol(T.xs, c), True, True).then_inc(sem["%s%d" % (nm, c)], 1)
     by_slot = sorted(near, key=lambda q: P["slot"][(q, rank)])
-    terms = (["own", 0, 1] if early else [0, 1, "own"])
+    terms = ["own", 0, 1]
     for t, what in enumerate(terms):
         if what == "own":
             PE.wait_ge(sem["qx%d" % rank], 1)
-            wq, ws, xq, xs = T.w1q, T.w1s, xcol(T.xq, rank), xcol(T.xs, rank)
-            w0 = 0
+            wq, ws, xq, xs = T.nq, T.ns, xcol(T.xq, rank), xcol(T.xs, rank)
+            w0 = NC
         else:
-            PE.wait_ge(sem.aw, sum(2 * _cnt(topo.mask(cores[q], core)) for q in near))
-            PE.wait_ge(sem["ax%d" % what], 2 * _cnt(topo.mask(cores[by_slot[what]], core)))
-            wq, ws, xq, xs = T.rwq, T.rws, xcol(T.rxq, what), xcol(T.rxs, what)
-            w0 = 256 * what
+            q = by_slot[what]
+            PE.wait_ge(sem.aw, sum(2 * _cnt(topo.mask(P["helpers"][ch][P["local"][ch].index(p)], core)) for p in near))
+            PE.wait_ge(sem["ax%d" % what], 2 * _cnt(topo.mask(cores[q], core)))
+            x0 = what * (NC + NW)
+            w0 = x0 + NC
+            wq, ws, xq, xs = T.rq, T.rs, T.rq[:, x0:x0 + NC], T.rs[:, x0:x0 + NC]
         for i, nm in enumerate(("mza", "mzb")):
             mm = PE.matmul_mx(bank(6 + i), wq[:, w0 + 128 * i:w0 + 128 * (i + 1)], ws[:, w0 + 128 * i:w0 + 128 * (i + 1)],
                               xq, xs, t == 0, t == 2)
@@ -226,10 +251,10 @@ def rank_program(g, core, T, topo):
     S.activation(T.yb[:, HC:NC], T.ps[:, (yp + 1) * NC:(yp + 1) * NC + HC], Copy).then_inc(sem.ye, 1)
 
     V.wait_ge(sem.lw1, 16)
-    V.quantize_mx(T.w1q[:], T.w1s[:], T.w1b[:]).then_inc(sem.qw1, 1)
+    V.quantize_mx(T.nq[:, NC:NC + NW], T.ns[:, NC:NC + NW], T.w1b[:]).then_inc(sem.qw1, 1)
     for c in order:
         V.wait_ge(sem["lx%d" % c], 16)
-        V.quantize_mx(xcol(T.xq, c), xcol(T.xs, c), T.xb[:, c * TW:(c + 1) * TW]).then_inc(sem["qx%d" % c], 1)
+        V.quantize_mx(tile(c)[0], tile(c)[1], T.xb[:, c * TW:(c + 1) * TW]).then_inc(sem["qx%d" % c], 1)
     fch = P["chip"][far[0]]
     for i, (nm, zn) in enumerate((("mza", "z0"), ("mzb", "z1"))):
         V.wait_ge(sem["far%d" % i], _cnt(topo.mask(P["jobs"][fch][(rank, i)][0], core)))
@@ -249,6 +274,10 @@ def rank_program(g, core, T, topo):
     loc = 0
     me = P["local"][ch].index(rank)
     ns = len(P["local"][ch])
+    g.wait_ge(sem.qw1, 1)
+    loc += _send(g, T, topo, core, P["helpers"][ch][me], _u8(T.hwq[:]), _u8(T.nq[:, NC:NC + NW]), sem.wr)
+    loc += _send(g, T, topo, core, P["helpers"][ch][me], T.hws[:], T.ns[:, NC:NC + NW], sem.wr)
+    g.sem_inc(sem.gate0, 1)
     for k, c in enumerate(far):
         g.wait_ge(sem["ev%d" % c], 2)
         trs = []
@@ -262,26 +291,19 @@ def rank_program(g, core, T, topo):
                 dst=T.fl[:, (sl * ns + me) * NC:(sl * ns + me + 1) * NC]))
             loc += _cnt(m)
         g.remote_dma_fused(trs, local_sem=sem.loc)
-    ids = [DstId(rid=topo.addr(cores[q])[0], pnc=topo.addr(cores[q])[1]) for q in near]
-    wm = topo.mask(core, cores[near[0]])
-    cols = [256 * P["slot"][(rank, q)] for q in near]
-    g.wait_ge(sem.qw1, 1)
-    g.remote_dma_fused([RemoteDMATransfer(dst_ids=ids, dma_engine_mask=wm, remote_sem=sem.aw, srcs=[_u8(T.w1q[:])],
-                                          dsts=[_u8(T.rwq[:, a:a + 256]) for a in cols])], local_sem=sem.loc)
-    g.remote_dma_fused([RemoteDMATransfer(dst_ids=ids, dma_engine_mask=wm, remote_sem=sem.aw, srcs=[T.w1s[:]],
-                                          dsts=[T.rws[:, a:a + 256] for a in cols])], local_sem=sem.loc)
-    loc += 2 * _cnt(wm)
+    g.sem_inc(sem.gatef, 1)
     for c in near:
         sl = P["slot"][(rank, c)]
+        b0 = sl * (NC + NW)
         g.wait_ge(sem["qx%d" % c], 1)
-        loc += _send(g, T, topo, core, cores[c], _u8(xcol(T.rxq, sl)), _u8(xcol(T.xq, c)), sem["ax%d" % sl])
-        loc += _send(g, T, topo, core, cores[c], xcol(T.rxs, sl), xcol(T.xs, c), sem["ax%d" % sl])
+        loc += _send(g, T, topo, core, cores[c], _u8(T.rq[:, b0:b0 + NC]), _u8(tile(c)[0]), sem["ax%d" % sl])
+        loc += _send(g, T, topo, core, cores[c], T.rs[:, b0:b0 + NC], tile(c)[1], sem["ax%d" % sl])
     g.sem_inc(sem.gate1, 1)
     g.wait_ge(sem.qh, 1)
     prv = (rank - 1) % n
     if topo.may_write(core, cores[prv]):
-        loc += _send(g, T, topo, core, cores[prv], T.rhs[:], T.hs[:], sem.ha)
         loc += _send(g, T, topo, core, cores[prv], _u8(T.rhq[:]), _u8(T.hq[:]), sem.ha)
+        loc += _send(g, T, topo, core, cores[prv], T.rhs[:], T.hs[:], sem.ha)
     else:
         hs = P["helpers"][ch]
         trs = []

@@ -8,6 +8,8 @@ HC = NC // 2
 NW = 256
 TW = 4 * NC
 CONST = 0.01674
+HV = ((0, HC), (HC, NC))
+AB = "ab"
 
 SCRATCH = {
     "xb": ("sbuf", [128, NR * TW], "bfloat16"),
@@ -37,11 +39,11 @@ SCRATCH = {
     "hws": ("sbuf", [128, NW], "uint8"),
     "ps": ("psum", [128, 8 * NC], "float32"),
 }
-SEMAPHORES = (["lw1", "lw2", "qw1", "qw2", "qh", "z0", "z1", "act", "ha", "mya", "myb", "ye", "yst", "hst",
-               "loc", "gate0", "gatef", "gate1", "gate2", "far0", "far1", "aw", "wr", "ax0", "ax1", "fj0", "fj1", "rl",
-               "mza", "mzb"]
-              + ["lx%d" % c for c in range(NR)] + ["qx%d" % c for c in range(NR)]
-              + ["ma%d" % c for c in range(NR)] + ["mb%d" % c for c in range(NR)] + ["ev%d" % c for c in range(NR)])
+SEMAPHORES = (["lw1", "lw2", "qw1", "qw2", "qha", "qhb", "z0a", "z0b", "z1a", "z1b", "acta", "actb", "ha", "haa", "hab",
+               "mya", "myb", "yea", "yeb", "yst", "hst", "loc", "gate0", "gatef", "gate1", "gate2",
+               "far0", "far1", "fbr0", "fbr1", "aw", "wr", "axa0", "axa1", "axb0", "axb1", "fj0", "fj1", "fk0", "fk1", "rl",
+               "eva", "evb", "mf00", "mf01", "mf10", "mf11", "mz00", "mz01", "mz10", "mz11"]
+              + ["%s%d" % (nm, c) for nm in ("lx", "la", "lb", "qx", "qa", "qb", "ma", "mb", "ev") for c in range(NR)])
 
 
 def _bits(m):
@@ -70,6 +72,7 @@ def _plan(T, topo):
     far = [sorted([d for d in range(n) if chip[d] != chip[r]], key=key) for r in range(n)]
     near = [sorted([d for d in range(n) if chip[d] == chip[r] and d != r], key=key) for r in range(n)]
     local, helpers, jobs = {}, {}, {}
+    fsplit = set()
     for ch in sorted(set(chip)):
         local[ch] = [r for r in range(n) if chip[r] == ch]
         away = [cores[r] for r in range(n) if chip[r] != ch]
@@ -86,6 +89,7 @@ def _plan(T, topo):
                     order.append(v.pop(0))
         helpers[ch] = order
         jobs[ch] = {}
+        fsplit.add(far[local[ch][0]][-1])
         for s, d in enumerate(far[local[ch][0]]):
             for i in range(2):
                 k = 2 * s + i
@@ -95,7 +99,14 @@ def _plan(T, topo):
         for k, q in enumerate(sorted(near[d], key=lambda q: (1 if q in prio else 0, q))):
             slot[(q, d)] = k
     return {"cores": cores, "n": n, "chip": chip, "prio": prio, "far": far, "near": near,
-            "local": local, "helpers": helpers, "jobs": jobs, "slot": slot}
+            "local": local, "helpers": helpers, "jobs": jobs, "slot": slot, "fsplit": fsplit}
+
+
+def _nmask(P, topo, q, d):
+    m = topo.mask(P["cores"][q], P["cores"][d])
+    if q in P["prio"]:
+        return _sub(m, P["near"][q].index(d), 2)
+    return m
 
 
 def _send(g, T, topo, src, dst, out, in_, sem):
@@ -130,20 +141,25 @@ def _helper(g, core, T, topo, P):
                                               dsts=[T.rs[:, a:a + NW] for a in cols])], local_sem=T.sem.loc)
         loc += 2 * _cnt(m)
     for sl, d, i in mine:
-        g.wait_ge(T.sem["fj%d" % sl], sum(_cnt(_sub(topo.mask(cores[q], core), i, 2)) for q in P["local"][ch]))
+        if d in P["fsplit"]:
+            parts = [(0, HC, "fj%d" % sl, "far%d" % i), (HC, NC, "fk%d" % sl, "fbr%d" % i)]
+        else:
+            parts = [(0, NC, "fj%d" % sl, "far%d" % i)]
         rid, pid, _se = topo.addr(cores[d])
         m = topo.mask(core, cores[d])
-        g.remote_dma_fused([RemoteDMATransfer(
-            dst_ids=[DstId(rid=rid, pnc=pid)], dma_engine_mask=m, remote_sem=T.sem["far%d" % i],
-            srcs=[T.fl[:, (sl * ns + q) * NC:(sl * ns + q + 1) * NC] for q in range(ns)],
-            dsts=[T.far[:, i * NC:(i + 1) * NC]], alu_op=1)], local_sem=T.sem.loc)
-        loc += _cnt(m)
+        for lo, hi, ws, rsm in parts:
+            g.wait_ge(T.sem[ws], sum(_cnt(_sub(topo.mask(cores[q], core), i, 2)) for q in P["local"][ch]))
+            g.remote_dma_fused([RemoteDMATransfer(
+                dst_ids=[DstId(rid=rid, pnc=pid)], dma_engine_mask=m, remote_sem=T.sem[rsm],
+                srcs=[T.fl[:, (sl * ns + q) * NC + lo:(sl * ns + q) * NC + hi] for q in range(ns)],
+                dsts=[T.far[:, i * NC + lo:i * NC + hi]], alu_op=1)], local_sem=T.sem.loc)
+            loc += _cnt(m)
     for s in sorted(P["prio"]):
         r = (s - 1) % P["n"]
         if P["chip"][s] != ch or topo.may_write(cores[s], cores[r]):
             continue
         if k < 2:
-            g.wait_ge(T.sem.rl, _cnt(_sub(topo.mask(cores[s], core), k, 2)))
+            g.wait_ge(T.sem.rl, _cnt(topo.mask(cores[s], core)))
             loc += _send(g, T, topo, core, cores[r], _u8(T.rhq[:, k * HC:(k + 1) * HC]),
                          _u8(T.relq[:, k * HC:(k + 1) * HC]), T.sem.ha)
         elif k == 2:
@@ -164,112 +180,166 @@ def rank_program(g, core, T, topo):
     sem, V, S, PE, SY = T.sem, g.vector, g.scalar, g.tensor, g.sync
     Copy, Relu = ActivationFunctionType.Copy, ActivationFunctionType.Relu
     fourth, rest = (rank, near) if early else (near[0], [near[1], rank])
-    order = far + [fourth] + rest
+    last = far[-1]
 
-    def bank(b):
-        return T.ps[:, b * NC:(b + 1) * NC]
+    def bank(b, w=NC):
+        return T.ps[:, b * NC:b * NC + w]
 
-    def xcol(t, c):
-        return t[:, c * NC:(c + 1) * NC]
-
-    def tile(c):
+    def tv(c, lo, hi):
         if c in near:
             a = near.index(c) * (NC + NW)
-            return T.nq[:, a:a + NC], T.ns[:, a:a + NC]
-        return xcol(T.xq, c), xcol(T.xs, c)
+            return T.nq[:, a + lo:a + hi], T.ns[:, a + lo:a + hi]
+        return T.xq[:, c * NC + lo:c * NC + hi], T.xs[:, c * NC + lo:c * NC + hi]
+
+    def qsem(c, h):
+        if c in rest or c == last:
+            return "q%s%d" % (AB[h], c)
+        return "qx%d" % c
+
+    def xbv(c, lo, hi):
+        return T.xb[:, c * TW + 4 * lo:c * TW + 4 * hi]
 
     SY.dma_start(T.w1b[:], T.w1[:, :]).then_inc(sem.lw1, 16)
-    for c in order:
-        if c == fourth:
-            SY.wait_ge(sem.gate0, 1)
-        if c == rest[0]:
-            SY.wait_ge(sem.gatef, 1)
-        SY.dma_start(T.xb[:, c * TW:(c + 1) * TW], T.x[:, c * TW:(c + 1) * TW]).then_inc(sem["lx%d" % c], 16)
+    for c in far:
+        SY.dma_start(xbv(c, 0, NC), T.x[:, c * TW:(c + 1) * TW]).then_inc(sem["lx%d" % c], 16)
+    SY.wait_ge(sem.gate0, 1)
+    SY.dma_start(xbv(fourth, 0, NC), T.x[:, fourth * TW:(fourth + 1) * TW]).then_inc(sem["lx%d" % fourth], 16)
+    SY.wait_ge(sem.gatef, 1)
+    for h, (lo, hi) in enumerate(HV):
+        for c in rest:
+            SY.dma_start(xbv(c, lo, hi), T.x[:, c * TW + 4 * lo:c * TW + 4 * hi]).then_inc(sem["l%s%d" % (AB[h], c)], 16)
     SY.wait_ge(sem.gate1, 1)
     SY.dma_start(T.w2b[:], T.w2[:, :]).then_inc(sem.lw2, 16)
     SY.wait_ge(sem.gate2, 1)
-    SY.wait_ge(sem.act, 4)
+    SY.wait_ge(sem.acta, 4)
+    SY.wait_ge(sem.actb, 4)
     SY.dma_start(T.h[:, :], T.hb[:]).then_inc(sem.hst, 16)
-    SY.wait_ge(sem.ye, 2)
-    SY.dma_start(T.y[:, :], T.yb[:]).then_inc(sem.yst, 16)
+    SY.wait_ge(sem.yea, 1)
+    SY.dma_start(T.y[:, 0:HC], T.yb[:, 0:HC]).then_inc(sem.yst, 16)
+    SY.wait_ge(sem.yeb, 1)
+    SY.dma_start(T.y[:, HC:NC], T.yb[:, HC:NC]).then_inc(sem.yst, 16)
     SY.wait_ge(sem.hst, 16)
-    SY.wait_ge(sem.yst, 16)
+    SY.wait_ge(sem.yst, 32)
+
+    def w1v(t, w0, i):
+        return t[:, w0 + 128 * i:w0 + 128 * (i + 1)]
 
     PE.wait_ge(sem.qw1, 1)
-    for k, c in enumerate(far):
+    for k, c in enumerate(far[:-1]):
         PE.wait_ge(sem["qx%d" % c], 1)
+        xq, xs = tv(c, 0, NC)
         for i, nm in enumerate(("ma", "mb")):
-            PE.matmul_mx(bank(2 * k + i), T.nq[:, NC + 128 * i:NC + 128 * (i + 1)], T.ns[:, NC + 128 * i:NC + 128 * (i + 1)],
-                         xcol(T.xq, c), xcol(T.xs, c), True, True).then_inc(sem["%s%d" % (nm, c)], 1)
+            PE.matmul_mx(bank(2 * k + i), w1v(T.nq, NC, i), w1v(T.ns, NC, i), xq, xs, True, True
+                         ).then_inc(sem["%s%d" % (nm, c)], 1)
+    for h, (lo, hi) in enumerate(HV):
+        PE.wait_ge(sem[qsem(last, h)], 1)
+        xq, xs = tv(last, lo, hi)
+        for i in range(2):
+            PE.matmul_mx(bank(4 + 2 * h + i, HC), w1v(T.nq, NC, i), w1v(T.ns, NC, i), xq, xs, True, True
+                         ).then_inc(sem["mf%d%d" % (h, i)], 1)
     by_slot = sorted(near, key=lambda q: P["slot"][(q, rank)])
-    terms = ["own", 0, 1]
-    for t, what in enumerate(terms):
-        if what == "own":
-            PE.wait_ge(sem["qx%d" % rank], 1)
-            wq, ws, xq, xs = T.nq, T.ns, xcol(T.xq, rank), xcol(T.xs, rank)
-            w0 = NC
-        else:
+    aw_all = sum(2 * _cnt(topo.mask(P["helpers"][ch][P["local"][ch].index(p)], core)) for p in near)
+    for c in far[:-1]:
+        PE.wait_ge(sem["ev%d" % c], 2)
+    for h, (lo, hi) in enumerate(HV):
+        PE.wait_ge(sem[qsem(rank, h)], 1)
+        xq, xs = tv(rank, lo, hi)
+        for i in range(2):
+            PE.matmul_mx(bank(2 * h + i, HC), w1v(T.nq, NC, i), w1v(T.ns, NC, i), xq, xs, True, False)
+    PE.wait_ge(sem.aw, aw_all)
+    for h, (lo, hi) in enumerate(HV):
+        for what in range(2):
             q = by_slot[what]
-            PE.wait_ge(sem.aw, sum(2 * _cnt(topo.mask(P["helpers"][ch][P["local"][ch].index(p)], core)) for p in near))
-            PE.wait_ge(sem["ax%d" % what], 2 * _cnt(topo.mask(cores[q], core)))
+            PE.wait_ge(sem["ax%s%d" % ("a" if early else AB[h], what)], 2 * _cnt(_nmask(P, topo, q, rank)))
             x0 = what * (NC + NW)
             w0 = x0 + NC
-            wq, ws, xq, xs = T.rq, T.rs, T.rq[:, x0:x0 + NC], T.rs[:, x0:x0 + NC]
-        for i, nm in enumerate(("mza", "mzb")):
-            mm = PE.matmul_mx(bank(6 + i), wq[:, w0 + 128 * i:w0 + 128 * (i + 1)], ws[:, w0 + 128 * i:w0 + 128 * (i + 1)],
-                              xq, xs, t == 0, t == 2)
-            if t == 2:
-                mm.then_inc(sem[nm], 1)
+            for i in range(2):
+                mm = PE.matmul_mx(bank(2 * h + i, HC), w1v(T.rq, w0, i), w1v(T.rs, w0, i),
+                                  T.rq[:, x0 + lo:x0 + hi], T.rs[:, x0 + lo:x0 + hi], False, what == 1)
+                if what == 1:
+                    mm.then_inc(sem["mz%d%d" % (h, i)], 1)
     yp = 4
-    PE.wait_ge(sem["ev%d" % far[2]], 2)
-    PE.wait_ge(sem.qh, 1)
+    PE.wait_ge(sem.eva, 2)
     PE.wait_ge(sem.qw2, 1)
-    for a in range(2):
-        PE.matmul_mx(T.ps[:, (yp + a) * NC:(yp + a) * NC + HC], T.w2q[:, 0:128], T.w2s[:, 0:128],
-                     T.hq[:, a * HC:(a + 1) * HC], T.hs[:, a * HC:(a + 1) * HC], True, False)
+    for a, (lo, hi) in enumerate(HV):
+        PE.wait_ge(sem["qh%s" % AB[a]], 1)
+        PE.matmul_mx(bank(yp + a, HC), T.w2q[:, 0:128], T.w2s[:, 0:128], T.hq[:, lo:hi], T.hs[:, lo:hi], True, False)
     nxt = (rank + 1) % n
-    if topo.may_write(cores[nxt], core):
-        h_in = 2 * _cnt(topo.mask(cores[nxt], core))
-    else:
-        h_in = sum(_cnt(topo.mask(hc, core)) for hc in P["helpers"][P["chip"][nxt]][:3])
-    PE.wait_ge(sem.ha, h_in)
-    for a, nm in enumerate(("mya", "myb")):
-        PE.matmul_mx(T.ps[:, (yp + a) * NC:(yp + a) * NC + HC], T.w2q[:, 128:256], T.w2s[:, 128:256],
-                     T.rhq[:, a * HC:(a + 1) * HC], T.rhs[:, a * HC:(a + 1) * HC], False, True).then_inc(sem[nm], 1)
+    direct_in = topo.may_write(cores[nxt], core)
+    for a, (lo, hi) in enumerate(HV):
+        if direct_in:
+            PE.wait_ge(sem["ha%s" % AB[a]], 2 * _cnt(topo.mask(cores[nxt], core)))
+        else:
+            PE.wait_ge(sem.ha, sum(_cnt(topo.mask(hc, core)) for hc in P["helpers"][P["chip"][nxt]][:3]))
+        PE.matmul_mx(bank(yp + a, HC), T.w2q[:, 128:256], T.w2s[:, 128:256], T.rhq[:, lo:hi], T.rhs[:, lo:hi], False, True
+                     ).then_inc(sem["my%s" % AB[a]], 1)
 
-    for k, c in enumerate(far):
+    for k, c in enumerate(far[:-1]):
         for i, nm in enumerate(("ma", "mb")):
             S.wait_ge(sem["%s%d" % (nm, c)], 1)
             S.activation(T.pout[:, (2 * k + i) * NC:(2 * k + i + 1) * NC], bank(2 * k + i), Copy
                          ).then_inc(sem["ev%d" % c], 1)
-    S.wait_ge(sem.z0, 1)
-    S.activation(T.hb[:, 0:TW:4], T.zb[:, 0:NC], Relu, scale=CONST).then_inc(sem.act, 1)
-    S.activation(T.hb[:, 1:TW:4], T.zb[:, 0:NC], Relu, scale=-CONST).then_inc(sem.act, 1)
-    S.wait_ge(sem.z1, 1)
-    S.activation(T.hb[:, 2:TW:4], T.zb[:, NC:2 * NC], Relu, scale=CONST).then_inc(sem.act, 1)
+    for h, (lo, hi) in enumerate(HV):
+        for i in range(2):
+            S.wait_ge(sem["mf%d%d" % (h, i)], 1)
+            S.activation(T.pout[:, (4 + i) * NC + lo:(4 + i) * NC + hi], bank(4 + 2 * h + i, HC), Copy
+                         ).then_inc(sem["ev%s" % AB[h]], 1)
+    for h, (lo, hi) in enumerate(HV):
+        act = sem["act%s" % AB[h]]
+        S.wait_ge(sem["z0%s" % AB[h]], 1)
+        S.activation(T.hb[:, 4 * lo + 0:4 * hi:4], T.zb[:, lo:hi], Relu, scale=CONST).then_inc(act, 1)
+        S.activation(T.hb[:, 4 * lo + 1:4 * hi:4], T.zb[:, lo:hi], Relu, scale=-CONST).then_inc(act, 1)
+        S.wait_ge(sem["z1%s" % AB[h]], 1)
+        S.activation(T.hb[:, 4 * lo + 2:4 * hi:4], T.zb[:, NC + lo:NC + hi], Relu, scale=CONST).then_inc(act, 1)
     S.wait_ge(sem.myb, 1)
-    S.activation(T.yb[:, HC:NC], T.ps[:, (yp + 1) * NC:(yp + 1) * NC + HC], Copy).then_inc(sem.ye, 1)
+    S.activation(T.yb[:, HC:NC], bank(yp + 1, HC), Copy).then_inc(sem.yeb, 1)
+
+    def quant(c, lo, hi, name):
+        q, s = tv(c, lo, hi)
+        V.quantize_mx(q, s, xbv(c, lo, hi)).then_inc(sem[name], 1)
 
     V.wait_ge(sem.lw1, 16)
     V.quantize_mx(T.nq[:, NC:NC + NW], T.ns[:, NC:NC + NW], T.w1b[:]).then_inc(sem.qw1, 1)
-    for c in order:
+    for c in far[:-1]:
         V.wait_ge(sem["lx%d" % c], 16)
-        V.quantize_mx(tile(c)[0], tile(c)[1], T.xb[:, c * TW:(c + 1) * TW]).then_inc(sem["qx%d" % c], 1)
+        quant(c, 0, NC, "qx%d" % c)
+    V.wait_ge(sem["lx%d" % last], 16)
+    for h, (lo, hi) in enumerate(HV):
+        quant(last, lo, hi, qsem(last, h))
+    V.wait_ge(sem["lx%d" % fourth], 16)
+    quant(fourth, 0, NC, "qx%d" % fourth)
+    for h, (lo, hi) in enumerate(HV):
+        for c in rest:
+            V.wait_ge(sem["l%s%d" % (AB[h], c)], 16)
+            quant(c, lo, hi, qsem(c, h))
     fch = P["chip"][far[0]]
-    for i, (nm, zn) in enumerate((("mza", "z0"), ("mzb", "z1"))):
-        V.wait_ge(sem["far%d" % i], _cnt(topo.mask(P["jobs"][fch][(rank, i)][0], core)))
-        V.wait_ge(sem[nm], 1)
-        V.tensor_tensor(T.zb[:, i * NC:(i + 1) * NC], bank(6 + i), T.far[:, i * NC:(i + 1) * NC],
-                        AluOpType.add).then_inc(sem[zn], 1)
-    V.wait_ge(sem.z1, 1)
-    V.tensor_scalar(T.hb[:, 3:TW:4], T.zb[:, NC:2 * NC], -CONST, 0.0, AluOpType.mult, AluOpType.max
-                    ).then_inc(sem.act, 1)
-    V.wait_ge(sem.act, 4)
-    V.quantize_mx(T.hq[:], T.hs[:], T.hb[:]).then_inc(sem.qh, 1)
+
+    def v_add(h):
+        lo, hi = HV[h]
+        for i in range(2):
+            fs = "fbr%d" % i if (rank in P["fsplit"] and h == 1) else "far%d" % i
+            V.wait_ge(sem[fs], _cnt(topo.mask(P["jobs"][fch][(rank, i)][0], core)))
+            V.wait_ge(sem["mz%d%d" % (h, i)], 1)
+            V.tensor_tensor(T.zb[:, i * NC + lo:i * NC + hi], bank(2 * h + i, HC), T.far[:, i * NC + lo:i * NC + hi],
+                            AluOpType.add).then_inc(sem["z%d%s" % (i, AB[h])], 1)
+
+    def v_rect(h):
+        lo, hi = HV[h]
+        V.wait_ge(sem["z1%s" % AB[h]], 1)
+        V.tensor_scalar(T.hb[:, 4 * lo + 3:4 * hi:4], T.zb[:, NC + lo:NC + hi], -CONST, 0.0, AluOpType.mult, AluOpType.max
+                        ).then_inc(sem["act%s" % AB[h]], 1)
+
+    def v_qh(h):
+        lo, hi = HV[h]
+        V.wait_ge(sem["act%s" % AB[h]], 4)
+        V.quantize_mx(T.hq[:, lo:hi], T.hs[:, lo:hi], T.hb[:, 4 * lo:4 * hi]).then_inc(sem["qh%s" % AB[h]], 1)
+
+    for fn, h in ((v_add, 0), (v_rect, 0), (v_add, 1), (v_qh, 0), (v_rect, 1), (v_qh, 1)):
+        fn(h)
     V.wait_ge(sem.lw2, 16)
     V.quantize_mx(T.w2q[:], T.w2s[:], T.w2b[:]).then_inc(sem.qw2, 1)
     V.wait_ge(sem.mya, 1)
-    V.tensor_copy(T.yb[:, 0:HC], T.ps[:, yp * NC:yp * NC + HC]).then_inc(sem.ye, 1)
+    V.tensor_copy(T.yb[:, 0:HC], bank(yp, HC)).then_inc(sem.yea, 1)
 
     loc = 0
     me = P["local"][ch].index(rank)
@@ -279,41 +349,66 @@ def rank_program(g, core, T, topo):
     loc += _send(g, T, topo, core, P["helpers"][ch][me], T.hws[:], T.ns[:, NC:NC + NW], sem.wr)
     g.sem_inc(sem.gate0, 1)
     for k, c in enumerate(far):
-        g.wait_ge(sem["ev%d" % c], 2)
-        trs = []
-        for i in range(2):
-            hc, sl = P["jobs"][ch][(c, i)]
-            rid, pid, _se = topo.addr(hc)
-            m = _sub(topo.mask(core, hc), i, 2)
-            trs.append(RemoteDMATransfer(
-                dst_ids=[DstId(rid=rid, pnc=pid)], dma_engine_mask=m, remote_sem=sem["fj%d" % sl],
-                src=T.pout[:, (2 * k + i) * NC:(2 * k + i + 1) * NC],
-                dst=T.fl[:, (sl * ns + me) * NC:(sl * ns + me + 1) * NC]))
-            loc += _cnt(m)
-        g.remote_dma_fused(trs, local_sem=sem.loc)
+        if c == last:
+            parts = [(0, HC, "eva", "fj"), (HC, NC, "evb", "fk")]
+        else:
+            parts = [(0, NC, "ev%d" % c, "fj")]
+        for lo, hi, ws, rsm in parts:
+            g.wait_ge(sem[ws], 2)
+            trs = []
+            for i in range(2):
+                hc, sl = P["jobs"][ch][(c, i)]
+                rid, pid, _se = topo.addr(hc)
+                m = _sub(topo.mask(core, hc), i, 2)
+                trs.append(RemoteDMATransfer(
+                    dst_ids=[DstId(rid=rid, pnc=pid)], dma_engine_mask=m, remote_sem=sem["%s%d" % (rsm, sl)],
+                    src=T.pout[:, (2 * k + i) * NC + lo:(2 * k + i) * NC + hi],
+                    dst=T.fl[:, (sl * ns + me) * NC + lo:(sl * ns + me) * NC + hi]))
+                loc += _cnt(m)
+            g.remote_dma_fused(trs, local_sem=sem.loc)
     g.sem_inc(sem.gatef, 1)
-    for c in near:
-        sl = P["slot"][(rank, c)]
-        b0 = sl * (NC + NW)
-        g.wait_ge(sem["qx%d" % c], 1)
-        loc += _send(g, T, topo, core, cores[c], _u8(T.rq[:, b0:b0 + NC]), _u8(tile(c)[0]), sem["ax%d" % sl])
-        loc += _send(g, T, topo, core, cores[c], T.rs[:, b0:b0 + NC], tile(c)[1], sem["ax%d" % sl])
+    if early:
+        for h, (lo, hi) in enumerate(HV):
+            for c in near:
+                g.wait_ge(sem[qsem(c, h)], 1)
+            for kind in range(2):
+                trs = []
+                for c in near:
+                    sl = P["slot"][(rank, c)]
+                    b0 = sl * (NC + NW)
+                    rid, pid, _se = topo.addr(cores[c])
+                    m = _nmask(P, topo, rank, c)
+                    q, s = tv(c, lo, hi)
+                    if kind == 0:
+                        src, dst = _u8(q), _u8(T.rq[:, b0 + lo:b0 + hi])
+                    else:
+                        src, dst = s, T.rs[:, b0 + lo:b0 + hi]
+                    trs.append(RemoteDMATransfer(dst_ids=[DstId(rid=rid, pnc=pid)], dma_engine_mask=m,
+                                                 remote_sem=sem["ax%s%d" % (AB[h], sl)], src=src, dst=dst))
+                    loc += _cnt(m)
+                g.remote_dma_fused(trs, local_sem=sem.loc)
+    else:
+        for c in near:
+            sl = P["slot"][(rank, c)]
+            b0 = sl * (NC + NW)
+            parts = [(0, 0, NC)] if c in P["prio"] else [(0, 0, HC), (1, HC, NC)]
+            for h, lo, hi in parts:
+                g.wait_ge(sem[qsem(c, h)], 1)
+                q, s = tv(c, lo, hi)
+                loc += _send(g, T, topo, core, cores[c], _u8(T.rq[:, b0 + lo:b0 + hi]), _u8(q), sem["ax%s%d" % (AB[h], sl)])
+                loc += _send(g, T, topo, core, cores[c], T.rs[:, b0 + lo:b0 + hi], s, sem["ax%s%d" % (AB[h], sl)])
     g.sem_inc(sem.gate1, 1)
-    g.wait_ge(sem.qh, 1)
     prv = (rank - 1) % n
     if topo.may_write(core, cores[prv]):
-        loc += _send(g, T, topo, core, cores[prv], _u8(T.rhq[:]), _u8(T.hq[:]), sem.ha)
-        loc += _send(g, T, topo, core, cores[prv], T.rhs[:], T.hs[:], sem.ha)
+        for h, (lo, hi) in enumerate(HV):
+            g.wait_ge(sem["qh%s" % AB[h]], 1)
+            loc += _send(g, T, topo, core, cores[prv], _u8(T.rhq[:, lo:hi]), _u8(T.hq[:, lo:hi]), sem["ha%s" % AB[h]])
+            loc += _send(g, T, topo, core, cores[prv], T.rhs[:, lo:hi], T.hs[:, lo:hi], sem["ha%s" % AB[h]])
     else:
         hs = P["helpers"][ch]
-        trs = []
-        for k in range(2):
-            rid, pid, _se = topo.addr(hs[k])
-            m = _sub(topo.mask(core, hs[k]), k, 2)
-            trs.append(RemoteDMATransfer(dst_ids=[DstId(rid=rid, pnc=pid)], dma_engine_mask=m, remote_sem=sem.rl,
-                                         src=_u8(T.hq[:, k * HC:(k + 1) * HC]), dst=_u8(T.relq[:, k * HC:(k + 1) * HC])))
-            loc += _cnt(m)
-        g.remote_dma_fused(trs, local_sem=sem.loc)
+        for h, (lo, hi) in enumerate(HV):
+            g.wait_ge(sem["qh%s" % AB[h]], 1)
+            loc += _send(g, T, topo, core, hs[h], _u8(T.relq[:, lo:hi]), _u8(T.hq[:, lo:hi]), sem.rl)
         loc += _send(g, T, topo, core, hs[2], T.rels[:], T.hs[:], sem.rl)
     g.sem_inc(sem.gate2, 1)
     g.wait_ge(sem.loc, loc)

from concourse.bass import DstId, RemoteDMATransfer
from concourse.mybir import dt, AluOpType, ActivationFunctionType

SIM_CORES = 16
NR = 6
NC = 512
HC = NC // 2
NW = 256
TW = 4 * NC
CONST = 0.01674
HV = ((0, HC), (HC, NC))
AB = "ab"

SCRATCH = {
    "xb": ("sbuf", [128, NR * TW], "bfloat16"),
    "xq": ("sbuf", [128, NR * NC], "float8_e4m3fn_x4"),
    "xs": ("sbuf", [128, NR * NC], "uint8"),
    "w1b": ("sbuf", [128, 1024], "bfloat16"),
    "nq": ("sbuf", [128, 2 * NC + NW], "float8_e4m3fn_x4"),
    "ns": ("sbuf", [128, 2 * NC + NW], "uint8"),
    "w2b": ("sbuf", [128, 1024], "bfloat16"),
    "w2q": ("sbuf", [128, 256], "float8_e4m3fn_x4"),
    "w2s": ("sbuf", [128, 256], "uint8"),
    "pout": ("sbuf", [128, 3 * 2 * NC], "float32"),
    "rq": ("sbuf", [128, 2 * (NC + NW)], "float8_e4m3fn_x4"),
    "rs": ("sbuf", [128, 2 * (NC + NW)], "uint8"),
    "far": ("sbuf", [128, 2 * NC], "float32"),
    "zb": ("sbuf", [128, 2 * NC], "float32"),
    "hb": ("sbuf", [128, TW], "bfloat16"),
    "hq": ("sbuf", [128, NC], "float8_e4m3fn_x4"),
    "hs": ("sbuf", [128, NC], "uint8"),
    "rhq": ("sbuf", [128, NC], "float8_e4m3fn_x4"),
    "rhs": ("sbuf", [128, NC], "uint8"),
    "yb": ("sbuf", [128, NC], "float32"),
    "fl": ("sbuf", [128, 2 * 3 * NC], "float32"),
    "relq": ("sbuf", [128, NC], "float8_e4m3fn_x4"),
    "rels": ("sbuf", [128, NC], "uint8"),
    "hwq": ("sbuf", [128, NW], "float8_e4m3fn_x4"),
    "hws": ("sbuf", [128, NW], "uint8"),
    "ps": ("psum", [128, 8 * NC], "float32"),
}
SEMAPHORES = (["lw1", "lw2", "qw1", "qw2", "qha", "qhb", "z0a", "z0b", "z1a", "z1b", "acta", "actb", "ha", "haa", "hab",
               "mya", "myb", "yea", "yeb", "yst", "hst", "loc", "gate0", "gatef", "gate1", "gate2",
               "far0", "far1", "fbr0", "fbr1", "aw", "wr", "axa0", "axa1", "axb0", "axb1", "fj0", "fj1", "fk0", "fk1", "rl",
               "eva", "evb", "mf00", "mf01", "mf10", "mf11", "mz00", "mz01", "mz10", "mz11"]
              + ["%s%d" % (nm, c) for nm in ("lx", "la", "lb", "qx", "qa", "qb", "ma", "mb", "ev") for c in range(NR)])


def _bits(m):
    return [b for b in range(m.bit_length()) if (m >> b) & 1]


def _cnt(m):
    return len(_bits(m))


def _sub(m, part, parts):
    bs = _bits(m)
    k = len(bs) // parts
    return sum(1 << b for b in bs[part * k:(part + 1) * k])


def _plan(T, topo):
    cores = [int(c) for c in T.cores]
    n = len(cores)
    chip = [topo.chip(c) for c in cores]
    prio = set((r + 1) % n for r in range(n) if chip[r] != chip[(r + 1) % n])

    def key(d):
        return (0 if d in prio else 1, d)

    far = [sorted([d for d in range(n) if chip[d] != chip[r]], key=key) for r in range(n)]
    near = [sorted([d for d in range(n) if chip[d] == chip[r] and d != r], key=key) for r in range(n)]
    local, helpers, jobs = {}, {}, {}
    fsplit = set()
    for ch in sorted(set(chip)):
        local[ch] = [r for r in range(n) if chip[r] == ch]
        away = [cores[r] for r in range(n) if chip[r] != ch]
        hs = [c for c in range(SIM_CORES) if topo.chip(c) == ch and c not in cores
              and all(topo.may_write(c, a) for a in away)]
        by = {}
        for c in hs:
            by.setdefault(topo.die(c), []).append(c)
        groups = sorted(by.values(), key=lambda v: -len(v))
        order = []
        while any(groups):
            for v in groups:
                if v:
                    order.append(v.pop(0))
        helpers[ch] = order
        jobs[ch] = {}
        fsplit.add(far[local[ch][0]][-1])
        for s, d in enumerate(far[local[ch][0]]):
            for i in range(2):
                k = 2 * s + i
                jobs[ch][(d, i)] = (order[k % len(order)], k // len(order))
    slot = {}
    for d in range(n):
        for k, q in enumerate(sorted(near[d], key=lambda q: (1 if q in prio else 0, q))):
            slot[(q, d)] = k
    return {"cores": cores, "n": n, "chip": chip, "prio": prio, "far": far, "near": near,
            "local": local, "helpers": helpers, "jobs": jobs, "slot": slot, "fsplit": fsplit}


def _nmask(P, topo, q, d):
    m = topo.mask(P["cores"][q], P["cores"][d])
    if q in P["prio"]:
        return _sub(m, P["near"][q].index(d), 2)
    return m


def _send(g, T, topo, src, dst, out, in_, sem):
    rid, pid, _se = topo.addr(dst)
    m = topo.mask(src, dst)
    g.remote_dma(out_ap=out, in_ap=in_, remote_sem=sem, local_sem=T.sem.loc, pid=pid, routing_id=rid, dma_engine_mask=m)
    return _cnt(m)


def _u8(view):
    return view.bitcast(dt.uint8)


def _helper(g, core, T, topo, P):
    ch = topo.chip(core)
    if core not in P["helpers"].get(ch, []):
        return
    cores, loc = P["cores"], 0
    mine = sorted([(sl, d, i) for (d, i), (h, sl) in P["jobs"][ch].items() if h == core])
    ns = len(P["local"][ch])
    k = P["helpers"][ch].index(core)
    if k < ns:
        q = P["local"][ch][k]
        g.wait_ge(T.sem.wr, 2 * _cnt(topo.mask(cores[q], core)))
        ds = P["near"][q]
        ids = [DstId(rid=topo.addr(cores[d])[0], pnc=topo.addr(cores[d])[1]) for d in ds]
        m = topo.mask(core, cores[ds[0]])
        cols = [P["slot"][(q, d)] * (NC + NW) + NC for d in ds]
        g.remote_dma_fused([RemoteDMATransfer(dst_ids=ids, dma_engine_mask=m, remote_sem=T.sem.aw, srcs=[_u8(T.hwq[:])],
                                              dsts=[_u8(T.rq[:, a:a + NW]) for a in cols])], local_sem=T.sem.loc)
        g.remote_dma_fused([RemoteDMATransfer(dst_ids=ids, dma_engine_mask=m, remote_sem=T.sem.aw, srcs=[T.hws[:]],
                                              dsts=[T.rs[:, a:a + NW] for a in cols])], local_sem=T.sem.loc)
        loc += 2 * _cnt(m)
    for sl, d, i in mine:
        if d in P["fsplit"]:
            parts = [(0, HC, "fj%d" % sl, "far%d" % i), (HC, NC, "fk%d" % sl, "fbr%d" % i)]
        else:
            parts = [(0, NC, "fj%d" % sl, "far%d" % i)]
        rid, pid, _se = topo.addr(cores[d])
        m = topo.mask(core, cores[d])
        for lo, hi, ws, rsm in parts:
            g.wait_ge(T.sem[ws], sum(_cnt(_sub(topo.mask(cores[q], core), i, 2)) for q in P["local"][ch]))
            g.remote_dma_fused([RemoteDMATransfer(
                dst_ids=[DstId(rid=rid, pnc=pid)], dma_engine_mask=m, remote_sem=T.sem[rsm],
                srcs=[T.fl[:, (sl * ns + q) * NC + lo:(sl * ns + q) * NC + hi] for q in range(ns)],
                dsts=[T.far[:, i * NC + lo:i * NC + hi]], alu_op=1)], local_sem=T.sem.loc)
            loc += _cnt(m)
    for s in sorted(P["prio"]):
        r = (s - 1) % P["n"]
        if P["chip"][s] != ch or topo.may_write(cores[s], cores[r]):
            continue
        if k < 2:
            g.wait_ge(T.sem.rl, _cnt(topo.mask(cores[s], core)))
            loc += _send(g, T, topo, core, cores[r], _u8(T.rhq[:, k * HC:(k + 1) * HC]),
                         _u8(T.relq[:, k * HC:(k + 1) * HC]), T.sem.ha)
        elif k == 2:
            g.wait_ge(T.sem.rl, _cnt(topo.mask(cores[s], core)))
            loc += _send(g, T, topo, core, cores[r], T.rhs[:], T.rels[:], T.sem.ha)
    g.wait_ge(T.sem.loc, loc)


def rank_program(g, core, T, topo):
    P = _plan(T, topo)
    rank = T.rank_of(core)
    if rank is None:
        _helper(g, core, T, topo, P)
        return
    cores, n, ch = P["cores"], P["n"], topo.chip(core)
    far, near = P["far"][rank], P["near"][rank]
    early = rank in P["prio"]
    sem, V, S, PE, SY = T.sem, g.vector, g.scalar, g.tensor, g.sync
    Copy, Relu = ActivationFunctionType.Copy, ActivationFunctionType.Relu
    fourth, rest = (rank, near) if early else (near[0], [near[1], rank])
    last = far[-1]

    def bank(b, w=NC):
        return T.ps[:, b * NC:b * NC + w]

    def tv(c, lo, hi):
        if c in near:
            a = near.index(c) * (NC + NW)
            return T.nq[:, a + lo:a + hi], T.ns[:, a + lo:a + hi]
        return T.xq[:, c * NC + lo:c * NC + hi], T.xs[:, c * NC + lo:c * NC + hi]

    def qsem(c, h):
        if c in rest or c == last:
            return "q%s%d" % (AB[h], c)
        return "qx%d" % c

    def xbv(c, lo, hi):
        return T.xb[:, c * TW + 4 * lo:c * TW + 4 * hi]

    SY.dma_start(T.w1b[:], T.w1[:, :]).then_inc(sem.lw1, 16)
    for c in far:
        SY.dma_start(xbv(c, 0, NC), T.x[:, c * TW:(c + 1) * TW]).then_inc(sem["lx%d" % c], 16)
    SY.wait_ge(sem.gate0, 1)
    SY.dma_start(xbv(fourth, 0, NC), T.x[:, fourth * TW:(fourth + 1) * TW]).then_inc(sem["lx%d" % fourth], 16)
    SY.wait_ge(sem.gatef, 1)
    for h, (lo, hi) in enumerate(HV):
        for c in rest:
            SY.dma_start(xbv(c, lo, hi), T.x[:, c * TW + 4 * lo:c * TW + 4 * hi]).then_inc(sem["l%s%d" % (AB[h], c)], 16)
    SY.wait_ge(sem.gate1, 1)
    SY.dma_start(T.w2b[:], T.w2[:, :]).then_inc(sem.lw2, 16)
    SY.wait_ge(sem.gate2, 1)
    SY.wait_ge(sem.acta, 4)
    SY.wait_ge(sem.actb, 4)
    SY.dma_start(T.h[:, :], T.hb[:]).then_inc(sem.hst, 16)
    SY.wait_ge(sem.yea, 1)
    SY.dma_start(T.y[:, 0:HC], T.yb[:, 0:HC]).then_inc(sem.yst, 16)
    SY.wait_ge(sem.yeb, 1)
    SY.dma_start(T.y[:, HC:NC], T.yb[:, HC:NC]).then_inc(sem.yst, 16)
    SY.wait_ge(sem.hst, 16)
    SY.wait_ge(sem.yst, 32)

    def w1v(t, w0, i):
        return t[:, w0 + 128 * i:w0 + 128 * (i + 1)]

    PE.wait_ge(sem.qw1, 1)
    for k, c in enumerate(far[:-1]):
        PE.wait_ge(sem["qx%d" % c], 1)
        xq, xs = tv(c, 0, NC)
        for i, nm in enumerate(("ma", "mb")):
            PE.matmul_mx(bank(2 * k + i), w1v(T.nq, NC, i), w1v(T.ns, NC, i), xq, xs, True, True
                         ).then_inc(sem["%s%d" % (nm, c)], 1)
    for h, (lo, hi) in enumerate(HV):
        PE.wait_ge(sem[qsem(last, h)], 1)
        xq, xs = tv(last, lo, hi)
        for i in range(2):
            PE.matmul_mx(bank(4 + 2 * h + i, HC), w1v(T.nq, NC, i), w1v(T.ns, NC, i), xq, xs, True, True
                         ).then_inc(sem["mf%d%d" % (h, i)], 1)
    by_slot = sorted(near, key=lambda q: P["slot"][(q, rank)])
    aw_all = sum(2 * _cnt(topo.mask(P["helpers"][ch][P["local"][ch].index(p)], core)) for p in near)
    for c in far[:-1]:
        PE.wait_ge(sem["ev%d" % c], 2)
    for h, (lo, hi) in enumerate(HV):
        PE.wait_ge(sem[qsem(rank, h)], 1)
        xq, xs = tv(rank, lo, hi)
        for i in range(2):
            PE.matmul_mx(bank(2 * h + i, HC), w1v(T.nq, NC, i), w1v(T.ns, NC, i), xq, xs, True, False)
    PE.wait_ge(sem.aw, aw_all)
    for h, (lo, hi) in enumerate(HV):
        for what in range(2):
            q = by_slot[what]
            PE.wait_ge(sem["ax%s%d" % ("a" if early else AB[h], what)], 2 * _cnt(_nmask(P, topo, q, rank)))
            x0 = what * (NC + NW)
            w0 = x0 + NC
            for i in range(2):
                mm = PE.matmul_mx(bank(2 * h + i, HC), w1v(T.rq, w0, i), w1v(T.rs, w0, i),
                                  T.rq[:, x0 + lo:x0 + hi], T.rs[:, x0 + lo:x0 + hi], False, what == 1)
                if what == 1:
                    mm.then_inc(sem["mz%d%d" % (h, i)], 1)
    yp = 4
    PE.wait_ge(sem.eva, 2)
    PE.wait_ge(sem.qw2, 1)
    for a, (lo, hi) in enumerate(HV):
        PE.wait_ge(sem["qh%s" % AB[a]], 1)
        PE.matmul_mx(bank(yp + a, HC), T.w2q[:, 0:128], T.w2s[:, 0:128], T.hq[:, lo:hi], T.hs[:, lo:hi], True, False)
    nxt = (rank + 1) % n
    direct_in = topo.may_write(cores[nxt], core)
    for a, (lo, hi) in enumerate(HV):
        if direct_in:
            PE.wait_ge(sem["ha%s" % AB[a]], 2 * _cnt(topo.mask(cores[nxt], core)))
        else:
            PE.wait_ge(sem.ha, sum(_cnt(topo.mask(hc, core)) for hc in P["helpers"][P["chip"][nxt]][:3]))
        PE.matmul_mx(bank(yp + a, HC), T.w2q[:, 128:256], T.w2s[:, 128:256], T.rhq[:, lo:hi], T.rhs[:, lo:hi], False, True
                     ).then_inc(sem["my%s" % AB[a]], 1)

    for k, c in enumerate(far[:-1]):
        for i, nm in enumerate(("ma", "mb")):
            S.wait_ge(sem["%s%d" % (nm, c)], 1)
            S.activation(T.pout[:, (2 * k + i) * NC:(2 * k + i + 1) * NC], bank(2 * k + i), Copy
                         ).then_inc(sem["ev%d" % c], 1)
    for h, (lo, hi) in enumerate(HV):
        for i in range(2):
            S.wait_ge(sem["mf%d%d" % (h, i)], 1)
            S.activation(T.pout[:, (4 + i) * NC + lo:(4 + i) * NC + hi], bank(4 + 2 * h + i, HC), Copy
                         ).then_inc(sem["ev%s" % AB[h]], 1)
    for h, (lo, hi) in enumerate(HV):
        act = sem["act%s" % AB[h]]
        S.wait_ge(sem["z0%s" % AB[h]], 1)
        S.activation(T.hb[:, 4 * lo + 0:4 * hi:4], T.zb[:, lo:hi], Relu, scale=CONST).then_inc(act, 1)
        S.activation(T.hb[:, 4 * lo + 1:4 * hi:4], T.zb[:, lo:hi], Relu, scale=-CONST).then_inc(act, 1)
        S.wait_ge(sem["z1%s" % AB[h]], 1)
        S.activation(T.hb[:, 4 * lo + 2:4 * hi:4], T.zb[:, NC + lo:NC + hi], Relu, scale=CONST).then_inc(act, 1)
    S.wait_ge(sem.myb, 1)
    S.activation(T.yb[:, HC:NC], bank(yp + 1, HC), Copy).then_inc(sem.yeb, 1)

    def quant(c, lo, hi, name):
        q, s = tv(c, lo, hi)
        V.quantize_mx(q, s, xbv(c, lo, hi)).then_inc(sem[name], 1)

    V.wait_ge(sem.lw1, 16)
    V.quantize_mx(T.nq[:, NC:NC + NW], T.ns[:, NC:NC + NW], T.w1b[:]).then_inc(sem.qw1, 1)
    for c in far[:-1]:
        V.wait_ge(sem["lx%d" % c], 16)
        quant(c, 0, NC, "qx%d" % c)
    V.wait_ge(sem["lx%d" % last], 16)
    for h, (lo, hi) in enumerate(HV):
        quant(last, lo, hi, qsem(last, h))
    V.wait_ge(sem["lx%d" % fourth], 16)
    quant(fourth, 0, NC, "qx%d" % fourth)
    for h, (lo, hi) in enumerate(HV):
        for c in rest:
            V.wait_ge(sem["l%s%d" % (AB[h], c)], 16)
            quant(c, lo, hi, qsem(c, h))
    fch = P["chip"][far[0]]

    def v_add(h):
        lo, hi = HV[h]
        for i in range(2):
            fs = "fbr%d" % i if (rank in P["fsplit"] and h == 1) else "far%d" % i
            V.wait_ge(sem[fs], _cnt(topo.mask(P["jobs"][fch][(rank, i)][0], core)))
            V.wait_ge(sem["mz%d%d" % (h, i)], 1)
            V.tensor_tensor(T.zb[:, i * NC + lo:i * NC + hi], bank(2 * h + i, HC), T.far[:, i * NC + lo:i * NC + hi],
                            AluOpType.add).then_inc(sem["z%d%s" % (i, AB[h])], 1)

    def v_rect(h):
        lo, hi = HV[h]
        V.wait_ge(sem["z1%s" % AB[h]], 1)
        V.tensor_scalar(T.hb[:, 4 * lo + 3:4 * hi:4], T.zb[:, NC + lo:NC + hi], -CONST, 0.0, AluOpType.mult, AluOpType.max
                        ).then_inc(sem["act%s" % AB[h]], 1)

    def v_qh(h):
        lo, hi = HV[h]
        V.wait_ge(sem["act%s" % AB[h]], 4)
        V.quantize_mx(T.hq[:, lo:hi], T.hs[:, lo:hi], T.hb[:, 4 * lo:4 * hi]).then_inc(sem["qh%s" % AB[h]], 1)

    for fn, h in ((v_add, 0), (v_rect, 0), (v_add, 1), (v_qh, 0), (v_rect, 1), (v_qh, 1)):
        fn(h)
    V.wait_ge(sem.lw2, 16)
    V.quantize_mx(T.w2q[:], T.w2s[:], T.w2b[:]).then_inc(sem.qw2, 1)
    V.wait_ge(sem.mya, 1)
    V.tensor_copy(T.yb[:, 0:HC], bank(yp, HC)).then_inc(sem.yea, 1)

    loc = 0
    me = P["local"][ch].index(rank)
    ns = len(P["local"][ch])
    g.wait_ge(sem.qw1, 1)
    loc += _send(g, T, topo, core, P["helpers"][ch][me], _u8(T.hwq[:]), _u8(T.nq[:, NC:NC + NW]), sem.wr)
    loc += _send(g, T, topo, core, P["helpers"][ch][me], T.hws[:], T.ns[:, NC:NC + NW], sem.wr)
    g.sem_inc(sem.gate0, 1)
    for k, c in enumerate(far):
        if c == last:
            parts = [(0, HC, "eva", "fj"), (HC, NC, "evb", "fk")]
        else:
            parts = [(0, NC, "ev%d" % c, "fj")]
        for lo, hi, ws, rsm in parts:
            g.wait_ge(sem[ws], 2)
            trs = []
            for i in range(2):
                hc, sl = P["jobs"][ch][(c, i)]
                rid, pid, _se = topo.addr(hc)
                m = _sub(topo.mask(core, hc), i, 2)
                trs.append(RemoteDMATransfer(
                    dst_ids=[DstId(rid=rid, pnc=pid)], dma_engine_mask=m, remote_sem=sem["%s%d" % (rsm, sl)],
                    src=T.pout[:, (2 * k + i) * NC + lo:(2 * k + i) * NC + hi],
                    dst=T.fl[:, (sl * ns + me) * NC + lo:(sl * ns + me) * NC + hi]))
                loc += _cnt(m)
            g.remote_dma_fused(trs, local_sem=sem.loc)
    g.sem_inc(sem.gatef, 1)
    if early:
        for h, (lo, hi) in enumerate(HV):
            for c in near:
                g.wait_ge(sem[qsem(c, h)], 1)
            for kind in range(2):
                trs = []
                for c in near:
                    sl = P["slot"][(rank, c)]
                    b0 = sl * (NC + NW)
                    rid, pid, _se = topo.addr(cores[c])
                    m = _nmask(P, topo, rank, c)
                    q, s = tv(c, lo, hi)
                    if kind == 0:
                        src, dst = _u8(q), _u8(T.rq[:, b0 + lo:b0 + hi])
                    else:
                        src, dst = s, T.rs[:, b0 + lo:b0 + hi]
                    trs.append(RemoteDMATransfer(dst_ids=[DstId(rid=rid, pnc=pid)], dma_engine_mask=m,
                                                 remote_sem=sem["ax%s%d" % (AB[h], sl)], src=src, dst=dst))
                    loc += _cnt(m)
                g.remote_dma_fused(trs, local_sem=sem.loc)
    else:
        for c in near:
            sl = P["slot"][(rank, c)]
            b0 = sl * (NC + NW)
            parts = [(0, 0, NC)] if c in P["prio"] else [(0, 0, HC), (1, HC, NC)]
            for h, lo, hi in parts:
                g.wait_ge(sem[qsem(c, h)], 1)
                q, s = tv(c, lo, hi)
                loc += _send(g, T, topo, core, cores[c], _u8(T.rq[:, b0 + lo:b0 + hi]), _u8(q), sem["ax%s%d" % (AB[h], sl)])
                loc += _send(g, T, topo, core, cores[c], T.rs[:, b0 + lo:b0 + hi], s, sem["ax%s%d" % (AB[h], sl)])
    g.sem_inc(sem.gate1, 1)
    prv = (rank - 1) % n
    if topo.may_write(core, cores[prv]):
        for h, (lo, hi) in enumerate(HV):
            g.wait_ge(sem["qh%s" % AB[h]], 1)
            loc += _send(g, T, topo, core, cores[prv], _u8(T.rhq[:, lo:hi]), _u8(T.hq[:, lo:hi]), sem["ha%s" % AB[h]])
            loc += _send(g, T, topo, core, cores[prv], T.rhs[:, lo:hi], T.hs[:, lo:hi], sem["ha%s" % AB[h]])
    else:
        hs = P["helpers"][ch]
        for h, (lo, hi) in enumerate(HV):
            g.wait_ge(sem["qh%s" % AB[h]], 1)
            loc += _send(g, T, topo, core, hs[h], _u8(T.relq[:, lo:hi]), _u8(T.hq[:, lo:hi]), sem.rl)
        loc += _send(g, T, topo, core, hs[2], T.rels[:], T.hs[:], sem.rl)
    g.sem_inc(sem.gate2, 1)
    g.wait_ge(sem.loc, loc)
